import numpy as np
import ml_dtypes


def mxq(x, axis, fmt="e4m3"):
    dtype, down = {"e4m3": (ml_dtypes.float8_e4m3fn, 7), "e5m2": (ml_dtypes.float8_e5m2, 14)}[fmt]
    v = np.moveaxis(np.asarray(x, np.float32).astype(ml_dtypes.bfloat16).astype(np.float64), axis, -1)
    blocks = v.reshape(v.shape[:-1] + (-1, 32))
    amax = np.abs(blocks).max(-1, keepdims=True)
    byte = np.maximum(np.where(amax > 0, np.frexp(amax)[1] - 1 + 127, 0) - down, 1)
    scale = np.exp2(byte - 127.0)
    codes = (blocks / scale).astype(np.float32).astype(dtype).astype(np.float64)
    return np.moveaxis((codes * scale).reshape(v.shape), -1, axis)


WIDE = False


def mx_kscale(k):
    if not WIDE:
        return np.ones(k)
    levels = np.array([10, -10, 5, -5, 0])
    if k % 512:
        return np.exp2(np.random.permutation(np.resize(levels, k // 32))).repeat(32)
    a = np.empty((k // 512, 16))
    for p in range(k // 512):
        a[p, :8] = np.random.permutation(np.resize(levels, 8))
        for g in range(8):
            far = levels[np.abs(levels - a[p, g]) >= 10]
            a[p, g + 8] = far[np.random.randint(len(far))]
    return np.exp2(a.ravel()).repeat(32)


BF16 = ml_dtypes.bfloat16


def bf(x):
    return np.asarray(x, np.float32).astype(BF16)


def f64(x):
    return np.asarray(x).astype(np.float64)


E2M1 = np.array([0.0, 0.5, 1.0, 1.5, 2.0, 3.0, 4.0, 6.0, -0.0, -0.5, -1.0, -1.5, -2.0, -3.0, -4.0, -6.0])


def pack_weight(w, fmt):
    k, n = w.shape
    w = f64(bf(w)).reshape(k // 32, 32, n)
    amax = np.abs(w).max(1)
    if fmt == "e4m3":
        byte = np.frexp(amax)[1] - 1 + 127 - 7
    else:
        mant, ex = np.frexp(amax / 6.0)
        byte = np.where(mant > 0.5, ex, ex - 1) + 127
    byte = np.clip(np.where(amax > 0, byte, 1), 1, 254)
    scaled = (w * np.exp2(127.0 - byte)[:, None, :]).reshape(k, n).astype(np.float32)
    by_word = np.ascontiguousarray(scaled.reshape(k // 512, 128, 4, n).transpose(0, 1, 3, 2))
    if fmt == "e4m3":
        words = by_word.astype(ml_dtypes.float8_e4m3fn).view(np.uint8)
    else:
        c = by_word.astype(ml_dtypes.float4_e2m1fn).view(np.uint8) & 0xF
        words = c[..., 0::2] | (c[..., 1::2] << 4)
    return np.ascontiguousarray(words), np.ascontiguousarray(byte.astype(np.uint8).reshape(k // 512, 16, n))


def unpack_weight(words, scales, fmt):
    g, p, n, _ = words.shape
    if fmt == "e4m3":
        vals = np.ascontiguousarray(words).view(ml_dtypes.float8_e4m3fn).astype(np.float64)
    else:
        nib = np.empty((g, p, n, 4), np.uint8)
        nib[..., 0::2] = words & 0xF
        nib[..., 1::2] = words >> 4
        vals = E2M1[nib]
    vals = vals * np.repeat(np.exp2(scales.astype(np.float64) - 127.0), 8, axis=1)[..., None]
    return vals.transpose(0, 1, 3, 2).reshape(g * 512, n)
def pack4(w):
    words, scales = pack_weight(w, "e2m1")
    return words.reshape(words.shape[0], 128, -1), scales


def unpack4(words, scales):
    return unpack_weight(words.reshape(words.shape[0], 128, -1, 2), scales, "e2m1")


def planes(Y):
    n, m = Y.shape
    b = f64(bf(Y)).reshape(n // 32, 32, m)
    amax = np.abs(b).max(1)
    byte = np.clip(np.where(amax > 0, np.frexp(amax)[1] - 1 + 127 - 7, 1), 1, 254)
    codes = (b * np.exp2(127.0 - byte)[:, None, :]).reshape(n, m).astype(np.float32).astype(ml_dtypes.float8_e4m3fn).view(np.uint8)
    words = codes.reshape(n // 512, 128, 4, m).transpose(0, 1, 3, 2)
    return np.ascontiguousarray(words), np.ascontiguousarray(byte.astype(np.uint8).reshape(n // 512, 16, m))


SUBS, OLD, TRAIN, TEST = 2048, 6144, 1024, 1024

def setup_inputs():
    s = mx_kscale(SUBS)
    t = mx_kscale(TRAIN)
    rate = 0.25 + 0.5 * np.random.rand(TRAIN)
    A = (np.random.rand(OLD + SUBS, TRAIN) < rate) * 1.0
    A = A - A.mean(axis=0)
    sd = A.std(axis=0)
    A = A / (sd * np.sqrt(OLD + SUBS))
    effect = 0.5 * np.exp(0.8 * np.random.randn(TRAIN, 1)) * np.random.randn(TRAIN, TEST)
    G = A @ effect + 0.1 * np.random.randn(OLD + SUBS, TEST)
    G = G - G.mean(axis=0)
    E = A.T @ A - np.eye(TRAIN)
    C_words, C_scales = pack4(E * t[None, :] / t[:, None])
    return {
        "Z": bf(A[OLD:] * s[:, None] * t[None, :]),
        "F": bf(G[OLD:] / s[:, None]),
        "B_old": bf((A[:OLD].T @ G[:OLD]) * t[:, None]),
        "C_words": C_words,
        "C_scales": C_scales,
        "inv_sd": bf(1.0 / (sd * t)),
    }

def reference(Z, F, B_old, C_words, C_scales, inv_sd):
    C = unpack4(C_words, C_scales)
    B = f64(B_old) + (mxq(f64(Z), 0, "e4m3").T @ mxq(f64(F), 0, "e4m3"))
    H = B - (C.T @ mxq(B, 0, "e4m3"))
    R = B - (C.T @ mxq(H, 0, "e4m3"))
    y = R * f64(inv_sd)[:, None]
    Y = y.reshape(TRAIN, TEST)
    words, scales = planes(Y)
    return y, words, scales

@@ -1,0 +1,486 @@
+from contextlib import ExitStack
+
+import concourse.mybir as mybir
+
+SUBS, TRAIN, TEST = 2048, 1024, 1024
+FLOPS = 2 * SUBS * TRAIN * TEST + 2 * 2 * TRAIN * TRAIN * TEST
+
+F32 = mybir.dt.float32
+BF16 = mybir.dt.bfloat16
+I32 = mybir.dt.int32
+U32 = mybir.dt.uint32
+U16 = mybir.dt.uint16
+U8 = mybir.dt.uint8
+FP8X4 = mybir.dt.float8_e4m3fn_x4
+FP4X4 = mybir.dt.float4_e2m1fn_x4
+ALU = mybir.AluOpType
+ACT = mybir.ActivationFunctionType
+
+P = 128
+PACK = 4
+GROUP = P * PACK
+SUB_PASSES = SUBS // GROUP
+GROUPS = TRAIN // GROUP
+CHUNK = 256
+CHUNKS = TEST // CHUNK
+HALF = 128
+LOAD_COLS = 512
+RAW_BUFS = 15
+
+
+def tile_datamodel_neumann_regression_k1_kernel(tc, Z, F, B_old, C_words, C_scales, inv_sd, out_0, out_1, out_2):
+    nc = tc.nc
+    with ExitStack() as ctx:
+        keep = ctx.enter_context(tc.tile_pool(name="keep", bufs=1))
+        raw = ctx.enter_context(tc.tile_pool(name="raw", bufs=1))
+        work = ctx.enter_context(tc.tile_pool(name="work", bufs=2))
+        psum = ctx.enter_context(tc.psum_pool(name="psum", bufs=8))
+        ctx.enter_context(tc.manual_schedule())
+
+        c_words_raw = keep.tile([P, GROUPS, 2 * TRAIN], U8, name="c_words_raw")
+        c_scales_raw = keep.tile([P, GROUPS, TRAIN], U8, name="c_scales_raw")
+        c_words = keep.tile([P, GROUPS, 2 * TRAIN], U8, name="c_words", align_bytes=64)
+        c_scales = keep.tile([P, GROUPS, TRAIN], U8, name="c_scales", align_bytes=64)
+        gain_raw = keep.tile([P, GROUPS, PACK], BF16, name="gain_raw")
+        gain = keep.tile([P, GROUPS * PACK], F32, name="gain")
+        minus_gain = keep.tile([P, GROUPS * PACK], F32, name="minus_gain")
+        y_scales = keep.tile([P, GROUPS, TEST], U8, name="y_scales", align_bytes=64)
+
+        b_all = keep.tile([P, GROUPS, PACK, TEST], F32, name="b_all")
+        z_raw, f_raw, b_old = {}, {}, {}
+        z_mx, f_mx, f_il, b_mx, h_mx = {}, {}, {}, {}, {}
+        z_il, banks, b_f32, y_f32, b_il, h_il, y_il, y_codes = {}, {}, {}, {}, {}, {}, {}, {}
+
+        for c in range(CHUNKS):
+            b_f32[c] = b_all[:, :, :, c * CHUNK : (c + 1) * CHUNK]
+
+        def load_rows(src, group, half):
+            tile = raw.tile([P, PACK, LOAD_COLS], BF16, name="rows", bufs=RAW_BUFS)
+            block = src[group * GROUP : (group + 1) * GROUP, half * LOAD_COLS : (half + 1) * LOAD_COLS]
+            nc.sync.dma_start(out=tile[:], in_=block.rearrange("(p j) n -> p j n", j=PACK))
+            return tile
+
+        def load_z(kp, g):
+            z_raw[kp, g] = load_rows(Z, kp, g)
+
+        def load_f(half, kp):
+            f_raw[half, kp] = load_rows(F, kp, half)
+
+        def load_b_old(half, g):
+            b_old[half, g] = load_rows(B_old, g, half)
+
+        def copy_on(on_vector, out, in_):
+            if on_vector:
+                nc.vector.tensor_copy(out=out, in_=in_)
+            else:
+                nc.scalar.copy(out=out, in_=in_)
+
+        def interleave(on_vector, out, in_):
+            copy_on(on_vector, out.rearrange("p (c i) t -> p c t i", i=2), in_.rearrange("p t (c i) -> p c t i", i=2))
+
+        def quantize(src, name, bufs):
+            width = src.shape[1]
+            codes = work.tile([P, width], U32, name=name + "_codes", bufs=bufs, align_bytes=64)
+            scales = work.tile([P, width], U8, name=name + "_scales", bufs=bufs, align_bytes=64)
+            nc.vector.quantize_mx(out=codes[:].bitcast(FP8X4), scales=scales[:], in_=src.rearrange("p n t -> p (n t)"))
+            return codes, scales
+
+        def interleave_z(kp, g, split):
+            z_il[kp, g] = work.tile([P, GROUP, PACK], BF16, name="z_il", bufs=5, align_bytes=64)
+            out = z_il[kp, g][:].rearrange("p (t m i) j -> p t m j i", t=PACK, i=2)
+            in_ = z_raw[kp, g][:].rearrange("p j (m i t) -> p t m j i", t=PACK, i=2)
+            if split < PACK:
+                nc.scalar.copy(out=out[:, split:], in_=in_[:, split:])
+            if split:
+                nc.vector.tensor_copy(out=out[:, :split], in_=in_[:, :split])
+
+        def quantize_z(kp, g):
+            z_mx[kp, g] = quantize(z_il[kp, g][:], "z", 12)
+
+        def interleave_f(c, kp, share=0):
+            f_il[c, kp] = work.tile([P, CHUNK, PACK], BF16, name="f_il", bufs=4, align_bytes=64)
+            first = c * CHUNK % LOAD_COLS
+            interleave(share, f_il[c, kp][:], f_raw[c * CHUNK // LOAD_COLS, kp][:, :, first : first + CHUNK])
+
+        def quantize_f(c, kp):
+            f_mx[c, kp] = quantize(f_il[c, kp][:], "f", 8)
+
+        def interleave_f_head(kp, share):
+            f_il[0, kp] = work.tile([P, LOAD_COLS, PACK], BF16, name="z_il", bufs=5, align_bytes=64)
+            split = share * 128
+            if share < 4:
+                interleave(False, f_il[0, kp][:, split:], f_raw[0, kp][:, :, split:])
+            if split:
+                interleave(True, f_il[0, kp][:, :split], f_raw[0, kp][:, :, :split])
+
+        def quantize_f_head(kp):
+            f_mx[0, kp] = quantize(f_il[0, kp][:], "z", 12)
+
+        def mx_pass(out, lhs, lhs_scale, rhs, cols, start, stop):
+            nc.tensor.matmul_mx(out=out, lhsT=lhs, lhsT_scale=lhs_scale, rhs=rhs[0][:, cols].bitcast(FP8X4), rhs_scale=rhs[1][:, cols], start=start, stop=stop)
+
+        def z_pass(out, c, kp, g, t):
+            cols = slice(t * P, (t + 1) * P)
+            mx_pass(out, z_mx[kp, g][0][:, cols].bitcast(FP8X4), z_mx[kp, g][1][:, cols], f_mx[c, kp], slice(0, out.shape[1]), kp == 0, kp == SUB_PASSES - 1)
+
+        def c_group(out, g, t, rhs, first):
+            col = g * GROUP + t * P
+            for kg in range(GROUPS):
+                mx_pass(out, c_words[:, kg, 2 * col : 2 * (col + P)].bitcast(FP4X4), c_scales[:, kg, col : col + P],
+                        rhs, slice(first(kg), first(kg) + HALF), kg == 0, kg == GROUPS - 1)
+
+        def moments(c, b):
+            banks[1, c, b] = psum.tile([P, 2, CHUNK], F32, name="bank")
+            for i in range(2):
+                for kp in range(SUB_PASSES):
+                    z_pass(banks[1, c, b][:, i, :], c, kp, b // 2, 2 * (b % 2) + i)
+
+        def moments_head(kp, g):
+            for t in range(PACK):
+                if kp == 0:
+                    banks[0, g, t] = psum.tile([P, LOAD_COLS], F32, name="bank")
+                z_pass(banks[0, g, t][:], 0, kp, g, t)
+
+        def add_old_head(g, t):
+            nc.vector.tensor_tensor(out=b_all[:, g, t, :LOAD_COLS], in0=banks[0, g, t][:], in1=b_old[0, g][:, t, :], op=ALU.add)
+
+        def add_old_part(c, t):
+            cols = slice(c * CHUNK, (c + 1) * CHUNK)
+            nc.vector.tensor_tensor(out=b_all[:, 1, t, cols], in0=banks[0, 1, t][:, cols], in1=b_old[0, 1][:, t, cols], op=ALU.add)
+
+        def add_old(c, b):
+            first = c * CHUNK % LOAD_COLS
+            slots = slice(2 * (b % 2), 2 * (b % 2) + 2)
+            nc.vector.tensor_tensor(out=b_f32[c][:, b // 2, slots, :], in0=banks[1, c, b][:],
+                                    in1=b_old[c * CHUNK // LOAD_COLS, b // 2][:, slots, first : first + CHUNK], op=ALU.add)
+
+        def round_b(c, g, on_vector=False):
+            if c not in b_il:
+                b_il[c] = work.tile([P, GROUPS * CHUNK, PACK], BF16, name="b_il", align_bytes=64)
+            interleave(on_vector, b_il[c][:, g * CHUNK : (g + 1) * CHUNK, :], b_f32[c][:, g])
+
+        def quantize_b(c):
+            b_mx[c] = quantize(b_il[c][:], "b", 2)
+
+        def scale_b(c, g):
+            if c not in y_f32:
+                y_f32[c] = work.tile([P, GROUPS, PACK, CHUNK], F32, name="y_f32", bufs=3)
+            for t in range(PACK):
+                nc.scalar.activation(out=y_f32[c][:, g, t, :], in_=b_f32[c][:, g, t, :], func=ACT.Copy,
+                                     scale=gain[:, g * PACK + t : g * PACK + t + 1])
+
+        def first_step(c, b):
+            h, g = b // 2, b % 2
+            banks[2, c, b] = psum.tile([P, PACK, HALF], F32, name="bank")
+            for t in range(PACK):
+                c_group(banks[2, c, b][:, t, :], g, t, b_mx[c], lambda kg: kg * CHUNK + h * HALF)
+
+        def subtract_h(c, b):
+            h, g = b // 2, b % 2
+            if c not in h_il:
+                h_il[c] = work.tile([P, GROUPS * CHUNK, PACK], BF16, name="h_il", align_bytes=64)
+            first = g * CHUNK + h * HALF
+            nc.vector.tensor_tensor(
+                out=h_il[c][:, first : first + HALF, :].rearrange("p (c i) t -> p c t i", i=2),
+                in0=b_f32[c][:, g, :, h * HALF : (h + 1) * HALF].rearrange("p t (c i) -> p c t i", i=2),
+                in1=banks[2, c, b][:].rearrange("p t (c i) -> p c t i", i=2), op=ALU.subtract)
+
+        def quantize_h(c):
+            h_mx[c] = quantize(h_il[c][:], "h", 2)
+
+        def second_step(c, b):
+            banks[3, c, b] = psum.tile([P, 2, CHUNK], F32, name="bank")
+            for i in range(2):
+                for h in range(2):
+                    c_group(banks[3, c, b][:, i, h * HALF : (h + 1) * HALF], b // 2, 2 * (b % 2) + i, h_mx[c],
+                            lambda kg: kg * CHUNK + h * HALF)
+
+        def finish_y(c, b):
+            g = b // 2
+            for i in range(2):
+                t = 2 * (b % 2) + i
+                nc.vector.scalar_tensor_tensor(out=y_f32[c][:, g, t, :], in0=banks[3, c, b][:, i, :],
+                                               scalar=minus_gain[:, g * PACK + t : g * PACK + t + 1], in1=y_f32[c][:, g, t, :],
+                                               op0=ALU.mult, op1=ALU.add)
+
+        def store_y(c, g):
+            dst = out_0[g * GROUP : (g + 1) * GROUP, c * CHUNK : (c + 1) * CHUNK]
+            nc.sync.dma_start(out=dst.rearrange("(p t) m -> p t m", t=PACK), in_=y_f32[c][:, g])
+
+        def round_y(c, g, on_vector=False):
+            y_il[c, g] = work.tile([P, CHUNK, PACK], BF16, name="y_il", bufs=3, align_bytes=64)
+            interleave(on_vector, y_il[c, g][:], y_f32[c][:, g])
+
+        def quantize_y(c, g):
+            cols = slice(c * CHUNK, (c + 1) * CHUNK)
+            codes = work.tile([P, CHUNK], U32, name="y_codes", bufs=4, align_bytes=64)
+            nc.vector.quantize_mx(out=codes[:].bitcast(FP8X4), scales=y_scales[:, g, cols], in_=y_il[c, g][:].rearrange("p n t -> p (n t)"))
+            y_codes[c, g] = codes
+
+        def store_codes(c, g):
+            cols = slice(c * CHUNK, (c + 1) * CHUNK)
+            nc.sync.dma_start(out=out_1[g, :, cols, :].rearrange("p m t -> p (m t)").bitcast(I32), in_=y_codes[c, g][:].bitcast(I32))
+
+        def load_c_words():
+            nc.sync.dma_start(out=c_words_raw[:].bitcast(I32), in_=C_words.rearrange("g p b -> p g b").bitcast(I32))
+
+        def load_c_scales():
+            for q in range(4):
+                nc.sync.dma_start(out=c_scales_raw[32 * q : 32 * q + 4].bitcast(I32),
+                                  in_=C_scales[:, 4 * q : 4 * q + 4, :].rearrange("g r n -> r g n").bitcast(I32))
+
+        def load_gain():
+            nc.sync.dma_start(out=gain_raw[:], in_=inv_sd.rearrange("(g p t) -> p g t", g=GROUPS, t=PACK))
+
+        def deal_c_words():
+            nc.vector.tensor_copy(
+                out=c_words[:].bitcast(U16).rearrange("p k (g t m) -> p (k g) t m", g=GROUPS, t=PACK),
+                in_=c_words_raw[:].bitcast(U16).rearrange("p k (g m t) -> p (k g) t m", g=GROUPS, t=PACK))
+
+        def deal_c_scales():
+            nc.vector.tensor_copy(
+                out=c_scales[:].rearrange("p k (g t m) -> p (k g) t m", g=GROUPS, t=PACK),
+                in_=c_scales_raw[:].rearrange("p k (g m t) -> p (k g) t m", g=GROUPS, t=PACK))
+
+        def gains():
+            nc.vector.tensor_copy(out=gain[:], in_=gain_raw[:].rearrange("p g t -> p (g t)"))
+            nc.vector.tensor_scalar(out=minus_gain[:], in0=gain_raw[:].rearrange("p g t -> p (g t)"), scalar1=-1.0, scalar2=None, op0=ALU.mult)
+
+        nc.gpsimd.memset(c_scales_raw[:].rearrange("p g n -> p (g n)").bitcast(I32), 0)
+
+        def store_scales(first=0, last=CHUNKS):
+            cols = slice(first * CHUNK, last * CHUNK)
+            for q in range(4):
+                nc.sync.dma_start(out=out_2[:, 4 * q : 4 * q + 4, cols].rearrange("g r n -> r g n").bitcast(I32),
+                                  in_=y_scales[32 * q : 32 * q + 4, :, cols].bitcast(I32))
+
+        steps = {
+            "LCW": load_c_words, "LCS": load_c_scales, "LG": load_gain, "CW": deal_c_words, "CS": deal_c_scales, "G": gains,
+            "LZ": load_z, "LF": load_f, "LB": load_b_old, "ZI": interleave_z, "QZ": quantize_z, "FH": interleave_f_head, "QFH": quantize_f_head,
+            "M": moments_head, "FI": interleave_f, "QF": quantize_f, "SC": store_scales, "Sa": moments, "Sb": first_step, "Sc": second_step,
+            "AH": add_old_head, "AG": add_old_part, "A": add_old, "BI": round_b, "QB": quantize_b, "BS": scale_b, "H": subtract_h, "QH": quantize_h,
+            "Y": finish_y, "YI": round_y, "QY": quantize_y, "SY": store_y, "SQ": store_codes,
+        }
+        steps["LF"](0, 0)
+        steps["LZ"](0, 0)
+        steps["LF"](0, 1)
+        steps["LZ"](1, 0)
+        steps["LCS"]()
+        steps["LF"](0, 2)
+        steps["LZ"](2, 0)
+        steps["LF"](0, 3)
+        steps["LZ"](3, 0)
+        steps["LCW"]()
+        steps["LZ"](0, 1)
+        steps["LZ"](1, 1)
+        steps["LZ"](2, 1)
+        steps["LZ"](3, 1)
+        steps["LB"](0, 0)
+        steps["LB"](0, 1)
+        steps["LF"](1, 0)
+        steps["LG"]()
+        steps["FH"](0, 2)
+        steps["LF"](1, 1)
+        steps["ZI"](0, 0, 2)
+        steps["LF"](1, 2)
+        steps["QFH"](0)
+        steps["FH"](1, 2)
+        steps["LF"](1, 3)
+        steps["QZ"](0, 0)
+        steps["M"](0, 0)
+        steps["ZI"](1, 0, 2)
+        steps["LB"](1, 0)
+        steps["QFH"](1)
+        steps["FH"](2, 1)
+        steps["LB"](1, 1)
+        steps["QZ"](1, 0)
+        steps["M"](1, 0)
+        steps["CS"]()
+        steps["ZI"](2, 0, 1)
+        steps["QFH"](2)
+        steps["FH"](3, 2)
+        steps["QZ"](2, 0)
+        steps["M"](2, 0)
+        steps["ZI"](3, 0, 1)
+        steps["QFH"](3)
+        steps["CW"]()
+        steps["ZI"](0, 1, 1)
+        steps["QZ"](3, 0)
+        steps["M"](3, 0)
+        steps["ZI"](1, 1, 2)
+        steps["QZ"](0, 1)
+        steps["M"](0, 1)
+        steps["ZI"](2, 1, 2)
+        steps["QZ"](1, 1)
+        steps["M"](1, 1)
+        steps["ZI"](3, 1, 2)
+        steps["QZ"](2, 1)
+        steps["M"](2, 1)
+        steps["AH"](0, 0)
+        steps["QZ"](3, 1)
+        steps["M"](3, 1)
+        steps["AH"](0, 1)
+        steps["AH"](0, 2)
+        steps["AH"](0, 3)
+        steps["BI"](0, 0)
+        steps["FI"](2, 0)
+        steps["BI"](1, 0)
+        steps["AG"](0, 0)
+        steps["AG"](0, 1)
+        steps["AG"](0, 2)
+        steps["AG"](0, 3)
+        steps["BI"](0, 1, 4)
+        steps["AG"](1, 0)
+        steps["AG"](1, 1)
+        steps["QB"](0)
+        steps["Sb"](0, 0)
+        steps["Sb"](0, 1)
+        steps["Sb"](0, 2)
+        steps["Sb"](0, 3)
+        steps["AG"](1, 2)
+        steps["AG"](1, 3)
+        steps["BI"](1, 1)
+        steps["FI"](2, 1)
+        steps["G"]()
+        steps["QF"](2, 0)
+        steps["FI"](2, 2)
+        steps["FI"](2, 3)
+        steps["H"](0, 0)
+        steps["QB"](1)
+        steps["Sb"](1, 0)
+        steps["Sb"](1, 1)
+        steps["Sb"](1, 2)
+        steps["Sb"](1, 3)
+        steps["H"](0, 1)
+        steps["QF"](2, 1)
+        steps["H"](0, 2)
+        steps["H"](0, 3)
+        steps["BS"](0, 0)
+        steps["BS"](0, 1)
+        steps["QF"](2, 2)
+        steps["H"](1, 0)
+        steps["QF"](2, 3)
+        steps["QH"](0)
+        steps["Sa"](2, 0)
+        steps["Sa"](2, 1)
+        steps["Sa"](2, 2)
+        steps["Sa"](2, 3)
+        steps["H"](1, 1)
+        steps["H"](1, 2)
+        steps["H"](1, 3)
+        steps["FI"](3, 0)
+        steps["FI"](3, 1)
+        steps["FI"](3, 2)
+        steps["FI"](3, 3)
+        steps["Sc"](0, 0)
+        steps["Sc"](0, 1)
+        steps["Sc"](0, 2)
+        steps["Sc"](0, 3)
+        steps["A"](2, 0)
+        steps["QH"](1)
+        steps["A"](2, 1)
+        steps["QF"](3, 0)
+        steps["QF"](3, 1)
+        steps["A"](2, 2)
+        steps["QF"](3, 2)
+        steps["A"](2, 3)
+        steps["BI"](2, 0)
+        steps["BI"](2, 1)
+        steps["QF"](3, 3)
+        steps["Sa"](3, 0)
+        steps["Sa"](3, 1)
+        steps["Sa"](3, 2)
+        steps["Sa"](3, 3)
+        steps["BS"](1, 0)
+        steps["BS"](1, 1)
+        steps["Y"](0, 0)
+        steps["Y"](0, 1)
+        steps["Y"](0, 2)
+        steps["Y"](0, 3)
+        steps["SY"](0, 0)
+        steps["SY"](0, 1)
+        steps["Sc"](1, 0)
+        steps["Sc"](1, 1)
+        steps["Sc"](1, 2)
+        steps["Sc"](1, 3)
+        steps["YI"](0, 0)
+        steps["YI"](0, 1)
+        steps["A"](3, 0)
+        steps["QB"](2)
+        steps["A"](3, 1)
+        steps["A"](3, 2)
+        steps["QY"](0, 0)
+        steps["SQ"](0, 0)
+        steps["A"](3, 3)
+        steps["BI"](3, 0)
+        steps["BI"](3, 1)
+        steps["Sb"](2, 0)
+        steps["Sb"](2, 1)
+        steps["Sb"](2, 2)
+        steps["Sb"](2, 3)
+        steps["Y"](1, 0)
+        steps["QY"](0, 1)
+        steps["SQ"](0, 1)
+        steps["Y"](1, 1)
+        steps["Y"](1, 2)
+        steps["Y"](1, 3)
+        steps["SY"](1, 0)
+        steps["SY"](1, 1)
+        steps["YI"](1, 0)
+        steps["YI"](1, 1)
+        steps["QB"](3)
+        steps["Sb"](3, 0)
+        steps["Sb"](3, 1)
+        steps["Sb"](3, 2)
+        steps["Sb"](3, 3)
+        steps["BS"](2, 0)
+        steps["BS"](2, 1)
+        steps["H"](2, 0)
+        steps["H"](2, 1)
+        steps["H"](2, 2)
+        steps["H"](2, 3)
+        steps["QY"](1, 0)
+        steps["QY"](1, 1)
+        steps["SQ"](1, 0)
+        steps["SQ"](1, 1)
+        steps["H"](3, 0)
+        steps["QH"](2)
+        steps["Sc"](2, 0)
+        steps["Sc"](2, 1)
+        steps["Sc"](2, 2)
+        steps["Sc"](2, 3)
+        steps["BS"](3, 0)
+        steps["BS"](3, 1)
+        steps["H"](3, 1)
+        steps["H"](3, 2)
+        steps["H"](3, 3)
+        steps["Y"](2, 0)
+        steps["QH"](3)
+        steps["Sc"](3, 0)
+        steps["Sc"](3, 1)
+        steps["Sc"](3, 2)
+        steps["Sc"](3, 3)
+        steps["Y"](2, 1)
+        steps["SY"](2, 0)
+        steps["YI"](2, 0)
+        steps["Y"](2, 2)
+        steps["Y"](2, 3)
+        steps["SY"](2, 1)
+        steps["YI"](2, 1)
+        steps["Y"](3, 0)
+        steps["Y"](3, 1)
+        steps["SY"](3, 0)
+        steps["QY"](2, 0)
+        steps["SQ"](2, 0)
+        steps["YI"](3, 0)
+        steps["Y"](3, 2)
+        steps["Y"](3, 3)
+        steps["SY"](3, 1)
+        steps["QY"](2, 1)
+        steps["SQ"](2, 1)
+        steps["YI"](3, 1, 4)
+        steps["QY"](3, 0)
+        steps["SQ"](3, 0)
+        steps["QY"](3, 1)
+        steps["SQ"](3, 1)
+        steps["SC"]()

@@ -25,6 +25,8 @@ CHUNK = 256
 CHUNKS = TEST // CHUNK
 HALF = 128
 LOAD_COLS = 512
+WIDE = 512
+RUN = 2
 RAW_BUFS = 15
 
 
@@ -76,7 +78,7 @@ def tile_datamodel_neumann_regression_k1_kernel(tc, Z, F, B_old, C_words, C_scal
                 nc.scalar.copy(out=out, in_=in_)
 
         def interleave(on_vector, out, in_):
-            copy_on(on_vector, out.rearrange("p (c i) t -> p c t i", i=2), in_.rearrange("p t (c i) -> p c t i", i=2))
+            copy_on(on_vector, out.rearrange("p (c i) t -> p c t i", i=RUN), in_.rearrange("p t (c i) -> p c t i", i=RUN))
 
         def quantize(src, name, bufs):
             width = src.shape[1]
@@ -98,7 +100,7 @@ def tile_datamodel_neumann_regression_k1_kernel(tc, Z, F, B_old, C_words, C_scal
             z_mx[kp, g] = quantize(z_il[kp, g][:], "z", 12)
 
         def interleave_f(c, kp, share=0):
-            f_il[c, kp] = work.tile([P, CHUNK, PACK], BF16, name="f_il", bufs=4, align_bytes=64)
+            f_il[c, kp] = work.tile([P, CHUNK, PACK], BF16, name="f_il", bufs=6, align_bytes=64)
             first = c * CHUNK % LOAD_COLS
             interleave(share, f_il[c, kp][:], f_raw[c * CHUNK // LOAD_COLS, kp][:, :, first : first + CHUNK])
 
@@ -156,18 +158,17 @@ def tile_datamodel_neumann_regression_k1_kernel(tc, Z, F, B_old, C_words, C_scal
 
         def round_b(c, g, on_vector=False):
             if c not in b_il:
-                b_il[c] = work.tile([P, GROUPS * CHUNK, PACK], BF16, name="b_il", align_bytes=64)
+                b_il[c] = work.tile([P, GROUPS * CHUNK, PACK], BF16, name="z_il", bufs=5, align_bytes=64)
             interleave(on_vector, b_il[c][:, g * CHUNK : (g + 1) * CHUNK, :], b_f32[c][:, g])
 
         def quantize_b(c):
             b_mx[c] = quantize(b_il[c][:], "b", 2)
 
-        def scale_b(c, g):
-            if c not in y_f32:
-                y_f32[c] = work.tile([P, GROUPS, PACK, CHUNK], F32, name="y_f32", bufs=3)
-            for t in range(PACK):
-                nc.scalar.activation(out=y_f32[c][:, g, t, :], in_=b_f32[c][:, g, t, :], func=ACT.Copy,
-                                     scale=gain[:, g * PACK + t : g * PACK + t + 1])
+        def scale_b(pair, g, t):
+            if t == 0:
+                y_f32[pair, g] = work.tile([P, PACK, WIDE], F32, name="y_f32", bufs=4)
+            nc.scalar.activation(out=y_f32[pair, g][:, t, :], in_=b_all[:, g, t, pair * WIDE : (pair + 1) * WIDE], func=ACT.Copy,
+                                 scale=gain[:, g * PACK + t : g * PACK + t + 1])
 
         def first_step(c, b):
             h, g = b // 2, b % 2
@@ -178,7 +179,7 @@ def tile_datamodel_neumann_regression_k1_kernel(tc, Z, F, B_old, C_words, C_scal
         def subtract_h(c, b):
             h, g = b // 2, b % 2
             if c not in h_il:
-                h_il[c] = work.tile([P, GROUPS * CHUNK, PACK], BF16, name="h_il", align_bytes=64)
+                h_il[c] = work.tile([P, GROUPS * CHUNK, PACK], BF16, name="z_il", bufs=5, align_bytes=64)
             first = g * CHUNK + h * HALF
             nc.vector.tensor_tensor(
                 out=h_il[c][:, first : first + HALF, :].rearrange("p (c i) t -> p c t i", i=2),
@@ -186,30 +187,37 @@ def tile_datamodel_neumann_regression_k1_kernel(tc, Z, F, B_old, C_words, C_scal
                 in1=banks[2, c, b][:].rearrange("p t (c i) -> p c t i", i=2), op=ALU.subtract)
 
         def quantize_h(c):
-            h_mx[c] = quantize(h_il[c][:], "h", 2)
+            if c % 2 == 0:
+                codes = work.tile([P, GROUPS, WIDE], U32, name="h_codes", align_bytes=64)
+                scales = work.tile([P, GROUPS, WIDE], U8, name="h_scales", align_bytes=64)
+                h_mx[c // 2] = codes, scales
+            codes, scales = h_mx[c // 2]
+            cols = slice(c % 2 * CHUNK, (c % 2 + 1) * CHUNK)
+            for g in range(GROUPS):
+                nc.vector.quantize_mx(out=codes[:, g, cols].bitcast(FP8X4), scales=scales[:, g, cols],
+                                      in_=h_il[c][:, g * CHUNK : (g + 1) * CHUNK, :].rearrange("p n t -> p (n t)"))
 
-        def second_step(c, b):
-            banks[3, c, b] = psum.tile([P, 2, CHUNK], F32, name="bank")
-            for i in range(2):
-                for h in range(2):
-                    c_group(banks[3, c, b][:, i, h * HALF : (h + 1) * HALF], b // 2, 2 * (b % 2) + i, h_mx[c],
-                            lambda kg: kg * CHUNK + h * HALF)
+        def second_step(pair, g, t):
+            banks[3, pair, g, t] = psum.tile([P, WIDE], F32, name="bank")
+            col = g * GROUP + t * P
+            codes, scales = h_mx[pair]
+            for kg in range(GROUPS):
+                nc.tensor.matmul_mx(out=banks[3, pair, g, t][:], lhsT=c_words[:, kg, 2 * col : 2 * (col + P)].bitcast(FP4X4),
+                                    lhsT_scale=c_scales[:, kg, col : col + P], rhs=codes[:, kg, :].bitcast(FP8X4),
+                                    rhs_scale=scales[:, kg, :], start=kg == 0, stop=kg == GROUPS - 1)
 
-        def finish_y(c, b):
-            g = b // 2
-            for i in range(2):
-                t = 2 * (b % 2) + i
-                nc.vector.scalar_tensor_tensor(out=y_f32[c][:, g, t, :], in0=banks[3, c, b][:, i, :],
-                                               scalar=minus_gain[:, g * PACK + t : g * PACK + t + 1], in1=y_f32[c][:, g, t, :],
-                                               op0=ALU.mult, op1=ALU.add)
+        def finish_y(pair, g, t):
+            nc.vector.scalar_tensor_tensor(out=y_f32[pair, g][:, t, :], in0=banks[3, pair, g, t][:],
+                                           scalar=minus_gain[:, g * PACK + t : g * PACK + t + 1], in1=y_f32[pair, g][:, t, :],
+                                           op0=ALU.mult, op1=ALU.add)
 
-        def store_y(c, g):
-            dst = out_0[g * GROUP : (g + 1) * GROUP, c * CHUNK : (c + 1) * CHUNK]
-            nc.sync.dma_start(out=dst.rearrange("(p t) m -> p t m", t=PACK), in_=y_f32[c][:, g])
+        def store_y(pair, g, t):
+            dst = out_0[g * GROUP : (g + 1) * GROUP, pair * WIDE : (pair + 1) * WIDE]
+            nc.sync.dma_start(out=dst.rearrange("(p t) m -> p t m", t=PACK)[:, t, :], in_=y_f32[pair, g][:, t, :])
 
         def round_y(c, g, on_vector=False):
-            y_il[c, g] = work.tile([P, CHUNK, PACK], BF16, name="y_il", bufs=3, align_bytes=64)
-            interleave(on_vector, y_il[c, g][:], y_f32[c][:, g])
+            y_il[c, g] = work.tile([P, CHUNK, PACK], BF16, name="f_il", bufs=6, align_bytes=64)
+            interleave(on_vector, y_il[c, g][:], y_f32[c // 2, g][:, :, c % 2 * CHUNK : (c % 2 + 1) * CHUNK])
 
         def quantize_y(c, g):
             cols = slice(c * CHUNK, (c + 1) * CHUNK)
@@ -246,12 +254,12 @@ def tile_datamodel_neumann_regression_k1_kernel(tc, Z, F, B_old, C_words, C_scal
             nc.vector.tensor_copy(out=gain[:], in_=gain_raw[:].rearrange("p g t -> p (g t)"))
             nc.vector.tensor_scalar(out=minus_gain[:], in0=gain_raw[:].rearrange("p g t -> p (g t)"), scalar1=-1.0, scalar2=None, op0=ALU.mult)
 
-        nc.gpsimd.memset(c_scales_raw[:].rearrange("p g n -> p (g n)").bitcast(I32), 0)
+        nc.vector.memset(c_scales_raw[:].rearrange("p g n -> p (g n)").bitcast(I32), 0)
 
         def store_scales(first=0, last=CHUNKS):
             cols = slice(first * CHUNK, last * CHUNK)
             for q in range(4):
-                nc.sync.dma_start(out=out_2[:, 4 * q : 4 * q + 4, cols].rearrange("g r n -> r g n").bitcast(I32),
+                nc.scalar.dma_start(out=out_2[:, 4 * q : 4 * q + 4, cols].rearrange("g r n -> r g n").bitcast(I32),
                                   in_=y_scales[32 * q : 32 * q + 4, :, cols].bitcast(I32))
 
         steps = {
@@ -270,15 +278,15 @@ def tile_datamodel_neumann_regression_k1_kernel(tc, Z, F, B_old, C_words, C_scal
         steps["LZ"](2, 0)
         steps["LF"](0, 3)
         steps["LZ"](3, 0)
-        steps["LCW"]()
         steps["LZ"](0, 1)
         steps["LZ"](1, 1)
         steps["LZ"](2, 1)
         steps["LZ"](3, 1)
         steps["LB"](0, 0)
+        steps["LCW"]()
         steps["LB"](0, 1)
-        steps["LF"](1, 0)
         steps["LG"]()
+        steps["LF"](1, 0)
         steps["FH"](0, 2)
         steps["LF"](1, 1)
         steps["ZI"](0, 0, 2)
@@ -291,20 +299,19 @@ def tile_datamodel_neumann_regression_k1_kernel(tc, Z, F, B_old, C_words, C_scal
         steps["ZI"](1, 0, 2)
         steps["LB"](1, 0)
         steps["QFH"](1)
-        steps["FH"](2, 1)
+        steps["FH"](2, 0)
         steps["LB"](1, 1)
         steps["QZ"](1, 0)
         steps["M"](1, 0)
         steps["CS"]()
-        steps["ZI"](2, 0, 1)
+        steps["ZI"](2, 0, 2)
         steps["QFH"](2)
         steps["FH"](3, 2)
         steps["QZ"](2, 0)
         steps["M"](2, 0)
-        steps["ZI"](3, 0, 1)
+        steps["ZI"](3, 0, 2)
         steps["QFH"](3)
-        steps["CW"]()
-        steps["ZI"](0, 1, 1)
+        steps["ZI"](0, 1, 2)
         steps["QZ"](3, 0)
         steps["M"](3, 0)
         steps["ZI"](1, 1, 2)
@@ -313,18 +320,18 @@ def tile_datamodel_neumann_regression_k1_kernel(tc, Z, F, B_old, C_words, C_scal
         steps["ZI"](2, 1, 2)
         steps["QZ"](1, 1)
         steps["M"](1, 1)
-        steps["ZI"](3, 1, 2)
+        steps["ZI"](3, 1, 0)
         steps["QZ"](2, 1)
         steps["M"](2, 1)
         steps["AH"](0, 0)
-        steps["QZ"](3, 1)
-        steps["M"](3, 1)
         steps["AH"](0, 1)
         steps["AH"](0, 2)
+        steps["QZ"](3, 1)
+        steps["M"](3, 1)
         steps["AH"](0, 3)
         steps["BI"](0, 0)
-        steps["FI"](2, 0)
         steps["BI"](1, 0)
+        steps["CW"]()
         steps["AG"](0, 0)
         steps["AG"](0, 1)
         steps["AG"](0, 2)
@@ -339,148 +346,165 @@ def tile_datamodel_neumann_regression_k1_kernel(tc, Z, F, B_old, C_words, C_scal
         steps["Sb"](0, 3)
         steps["AG"](1, 2)
         steps["AG"](1, 3)
-        steps["BI"](1, 1)
+        steps["FI"](2, 0)
         steps["FI"](2, 1)
-        steps["G"]()
-        steps["QF"](2, 0)
         steps["FI"](2, 2)
         steps["FI"](2, 3)
-        steps["H"](0, 0)
+        steps["FI"](3, 0)
+        steps["FI"](3, 1)
+        steps["G"]()
+        steps["BI"](1, 1, 4)
+        steps["QF"](2, 0)
+        steps["QF"](2, 1)
+        steps["FI"](3, 2)
+        steps["FI"](3, 3)
         steps["QB"](1)
         steps["Sb"](1, 0)
         steps["Sb"](1, 1)
         steps["Sb"](1, 2)
         steps["Sb"](1, 3)
+        steps["H"](0, 0)
         steps["H"](0, 1)
-        steps["QF"](2, 1)
+        steps["QF"](2, 2)
         steps["H"](0, 2)
         steps["H"](0, 3)
-        steps["BS"](0, 0)
-        steps["BS"](0, 1)
-        steps["QF"](2, 2)
-        steps["H"](1, 0)
         steps["QF"](2, 3)
-        steps["QH"](0)
         steps["Sa"](2, 0)
         steps["Sa"](2, 1)
         steps["Sa"](2, 2)
         steps["Sa"](2, 3)
+        steps["H"](1, 0)
+        steps["QH"](0)
         steps["H"](1, 1)
-        steps["H"](1, 2)
-        steps["H"](1, 3)
-        steps["FI"](3, 0)
-        steps["FI"](3, 1)
-        steps["FI"](3, 2)
-        steps["FI"](3, 3)
-        steps["Sc"](0, 0)
-        steps["Sc"](0, 1)
-        steps["Sc"](0, 2)
-        steps["Sc"](0, 3)
-        steps["A"](2, 0)
-        steps["QH"](1)
-        steps["A"](2, 1)
         steps["QF"](3, 0)
+        steps["H"](1, 2)
         steps["QF"](3, 1)
-        steps["A"](2, 2)
+        steps["H"](1, 3)
         steps["QF"](3, 2)
-        steps["A"](2, 3)
-        steps["BI"](2, 0)
-        steps["BI"](2, 1)
+        steps["A"](2, 0)
         steps["QF"](3, 3)
         steps["Sa"](3, 0)
+        steps["QH"](1)
+        steps["A"](2, 1)
         steps["Sa"](3, 1)
+        steps["BS"](0, 0, 0)
+        steps["BS"](0, 0, 1)
+        steps["BS"](0, 0, 2)
+        steps["BS"](0, 0, 3)
+        steps["A"](2, 2)
+        steps["BI"](2, 0)
         steps["Sa"](3, 2)
+        steps["A"](2, 3)
         steps["Sa"](3, 3)
-        steps["BS"](1, 0)
-        steps["BS"](1, 1)
-        steps["Y"](0, 0)
-        steps["Y"](0, 1)
-        steps["Y"](0, 2)
-        steps["Y"](0, 3)
-        steps["SY"](0, 0)
-        steps["SY"](0, 1)
-        steps["Sc"](1, 0)
-        steps["Sc"](1, 1)
-        steps["Sc"](1, 2)
-        steps["Sc"](1, 3)
-        steps["YI"](0, 0)
-        steps["YI"](0, 1)
+        steps["BI"](2, 1)
         steps["A"](3, 0)
-        steps["QB"](2)
         steps["A"](3, 1)
-        steps["A"](3, 2)
-        steps["QY"](0, 0)
-        steps["SQ"](0, 0)
-        steps["A"](3, 3)
+        steps["Sc"](0, 0, 0)
+        steps["Sc"](0, 0, 1)
+        steps["QB"](2)
         steps["BI"](3, 0)
+        steps["A"](3, 2)
+        steps["Sc"](0, 0, 2)
+        steps["A"](3, 3)
+        steps["Sc"](0, 0, 3)
         steps["BI"](3, 1)
+        steps["BS"](0, 1, 0)
+        steps["BS"](0, 1, 1)
+        steps["BS"](0, 1, 2)
+        steps["BS"](0, 1, 3)
         steps["Sb"](2, 0)
         steps["Sb"](2, 1)
         steps["Sb"](2, 2)
         steps["Sb"](2, 3)
-        steps["Y"](1, 0)
-        steps["QY"](0, 1)
-        steps["SQ"](0, 1)
-        steps["Y"](1, 1)
-        steps["Y"](1, 2)
-        steps["Y"](1, 3)
-        steps["SY"](1, 0)
-        steps["SY"](1, 1)
+        steps["Y"](0, 0, 0)
+        steps["SY"](0, 0, 0)
+        steps["Y"](0, 0, 1)
+        steps["SY"](0, 0, 1)
+        steps["Y"](0, 0, 2)
+        steps["SY"](0, 0, 2)
+        steps["Y"](0, 0, 3)
+        steps["SY"](0, 0, 3)
+        steps["YI"](0, 0)
         steps["YI"](1, 0)
-        steps["YI"](1, 1)
         steps["QB"](3)
         steps["Sb"](3, 0)
         steps["Sb"](3, 1)
         steps["Sb"](3, 2)
         steps["Sb"](3, 3)
-        steps["BS"](2, 0)
-        steps["BS"](2, 1)
+        steps["BS"](1, 0, 0)
+        steps["BS"](1, 0, 1)
+        steps["BS"](1, 0, 2)
+        steps["BS"](1, 0, 3)
+        steps["BS"](1, 1, 0)
+        steps["BS"](1, 1, 1)
+        steps["BS"](1, 1, 2)
+        steps["BS"](1, 1, 3)
         steps["H"](2, 0)
         steps["H"](2, 1)
         steps["H"](2, 2)
         steps["H"](2, 3)
-        steps["QY"](1, 0)
-        steps["QY"](1, 1)
-        steps["SQ"](1, 0)
-        steps["SQ"](1, 1)
+        steps["QY"](0, 0)
+        steps["SQ"](0, 0)
+        steps["Sc"](0, 1, 0)
+        steps["Sc"](0, 1, 1)
+        steps["Sc"](0, 1, 2)
+        steps["Sc"](0, 1, 3)
         steps["H"](3, 0)
         steps["QH"](2)
-        steps["Sc"](2, 0)
-        steps["Sc"](2, 1)
-        steps["Sc"](2, 2)
-        steps["Sc"](2, 3)
-        steps["BS"](3, 0)
-        steps["BS"](3, 1)
         steps["H"](3, 1)
+        steps["QY"](1, 0)
+        steps["SQ"](1, 0)
         steps["H"](3, 2)
         steps["H"](3, 3)
-        steps["Y"](2, 0)
+        steps["Y"](0, 1, 0)
+        steps["SY"](0, 1, 0)
         steps["QH"](3)
-        steps["Sc"](3, 0)
-        steps["Sc"](3, 1)
-        steps["Sc"](3, 2)
-        steps["Sc"](3, 3)
-        steps["Y"](2, 1)
-        steps["SY"](2, 0)
+        steps["Sc"](1, 0, 0)
+        steps["Sc"](1, 0, 1)
+        steps["Sc"](1, 0, 2)
+        steps["Sc"](1, 0, 3)
+        steps["Y"](0, 1, 1)
+        steps["SY"](0, 1, 1)
+        steps["Y"](0, 1, 2)
+        steps["SY"](0, 1, 2)
+        steps["Y"](0, 1, 3)
+        steps["SY"](0, 1, 3)
+        steps["Sc"](1, 1, 0)
+        steps["Sc"](1, 1, 1)
+        steps["Sc"](1, 1, 2)
+        steps["Sc"](1, 1, 3)
+        steps["YI"](0, 1)
+        steps["YI"](1, 1)
+        steps["Y"](1, 0, 0)
+        steps["SY"](1, 0, 0)
+        steps["Y"](1, 0, 1)
+        steps["SY"](1, 0, 1)
+        steps["Y"](1, 0, 2)
+        steps["SY"](1, 0, 2)
+        steps["Y"](1, 0, 3)
+        steps["SY"](1, 0, 3)
         steps["YI"](2, 0)
-        steps["Y"](2, 2)
-        steps["Y"](2, 3)
-        steps["SY"](2, 1)
-        steps["YI"](2, 1)
-        steps["Y"](3, 0)
-        steps["Y"](3, 1)
-        steps["SY"](3, 0)
+        steps["YI"](3, 0)
+        steps["QY"](0, 1)
+        steps["SQ"](0, 1)
+        steps["Y"](1, 1, 0)
+        steps["SY"](1, 1, 0)
+        steps["Y"](1, 1, 1)
+        steps["SY"](1, 1, 1)
+        steps["QY"](1, 1)
+        steps["SQ"](1, 1)
+        steps["Y"](1, 1, 2)
+        steps["SY"](1, 1, 2)
+        steps["Y"](1, 1, 3)
+        steps["SY"](1, 1, 3)
         steps["QY"](2, 0)
         steps["SQ"](2, 0)
-        steps["YI"](3, 0)
-        steps["Y"](3, 2)
-        steps["Y"](3, 3)
-        steps["SY"](3, 1)
-        steps["QY"](2, 1)
-        steps["SQ"](2, 1)
+        steps["YI"](2, 1)
         steps["YI"](3, 1, 4)
         steps["QY"](3, 0)
         steps["SQ"](3, 0)
         steps["QY"](3, 1)
         steps["SQ"](3, 1)
+        steps["QY"](2, 1)
+        steps["SQ"](2, 1)
         steps["SC"]()

@@ -17,24 +17,30 @@ ALU = mybir.AluOpType
 ACT = mybir.ActivationFunctionType
 
 P = 128
-PACK = 4
-GROUP = P * PACK
-SUB_PASSES = SUBS // GROUP
+SLOTS = 4
+GROUP = P * SLOTS
+PASSES = SUBS // GROUP
 GROUPS = TRAIN // GROUP
-CHUNK = 256
-CHUNKS = TEST // CHUNK
-HALF = 128
-LOAD_COLS = 512
 WIDE = 512
-RUN = 2
-RAW_BUFS = 15
+CHUNK = 256
+NARROW = 128
+BANKS = 4
+QUADRANTS = 4
+RUN = 4
+Z_RUN = 2
+EVEN_SHARE = 2
+ROW_TILES = 15
+WIDE_STAGES = 5
+NARROW_STAGES = 6
 
 
-def tile_datamodel_neumann_regression_k1_kernel(tc, Z, F, B_old, C_words, C_scales, inv_sd, out_0, out_1, out_2):
+def tile_datamodel_neumann_regression_k1_kernel(
+    tc, Z, F, B_old, C_words, C_scales, inv_sd, out_0, out_1, out_2
+):
     nc = tc.nc
     with ExitStack() as ctx:
         keep = ctx.enter_context(tc.tile_pool(name="keep", bufs=1))
-        raw = ctx.enter_context(tc.tile_pool(name="raw", bufs=1))
+        rows = ctx.enter_context(tc.tile_pool(name="rows", bufs=ROW_TILES))
         work = ctx.enter_context(tc.tile_pool(name="work", bufs=2))
         psum = ctx.enter_context(tc.psum_pool(name="psum", bufs=8))
         ctx.enter_context(tc.manual_schedule())
@@ -43,468 +49,307 @@ def tile_datamodel_neumann_regression_k1_kernel(tc, Z, F, B_old, C_words, C_scal
         c_scales_raw = keep.tile([P, GROUPS, TRAIN], U8, name="c_scales_raw")
         c_words = keep.tile([P, GROUPS, 2 * TRAIN], U8, name="c_words", align_bytes=64)
         c_scales = keep.tile([P, GROUPS, TRAIN], U8, name="c_scales", align_bytes=64)
-        gain_raw = keep.tile([P, GROUPS, PACK], BF16, name="gain_raw")
-        gain = keep.tile([P, GROUPS * PACK], F32, name="gain")
-        minus_gain = keep.tile([P, GROUPS * PACK], F32, name="minus_gain")
+        gain_raw = keep.tile([P, GROUPS, SLOTS], BF16, name="gain_raw")
+        gain = keep.tile([P, GROUPS * SLOTS], F32, name="gain")
+        minus_gain = keep.tile([P, GROUPS * SLOTS], F32, name="minus_gain")
         y_scales = keep.tile([P, GROUPS, TEST], U8, name="y_scales", align_bytes=64)
+        b_f32 = keep.tile([P, GROUPS, SLOTS, TEST], F32, name="b_f32")
 
-        b_all = keep.tile([P, GROUPS, PACK, TEST], F32, name="b_all")
-        z_raw, f_raw, b_old = {}, {}, {}
-        z_mx, f_mx, f_il, b_mx, h_mx = {}, {}, {}, {}, {}
-        z_il, banks, b_f32, y_f32, b_il, h_il, y_il, y_codes = {}, {}, {}, {}, {}, {}, {}, {}
+        z_rows, f_rows, b_old = {}, {}, {}
+        z_cols, f_cols, b_cols, h_cols, y_cols = {}, {}, {}, {}, {}
+        z_mx, f_mx, b_mx, h_mx = {}, {}, {}, {}
+        y_f32, banks = {}, {}
 
-        for c in range(CHUNKS):
-            b_f32[c] = b_all[:, :, :, c * CHUNK : (c + 1) * CHUNK]
+        def span(index, width):
+            return slice(index * width, (index + 1) * width)
 
-        def load_rows(src, group, half):
-            tile = raw.tile([P, PACK, LOAD_COLS], BF16, name="rows", bufs=RAW_BUFS)
-            block = src[group * GROUP : (group + 1) * GROUP, half * LOAD_COLS : (half + 1) * LOAD_COLS]
-            nc.sync.dma_start(out=tile[:], in_=block.rearrange("(p j) n -> p j n", j=PACK))
-            return tile
 
-        def load_z(kp, g):
-            z_raw[kp, g] = load_rows(Z, kp, g)
+        def load_rows(tiles, src, group, half):
+            tiles[group, half] = rows.tile([P, SLOTS, WIDE], BF16, name="rows")
+            block = src[span(group, GROUP), span(half, WIDE)]
+            nc.sync.dma_start(out=tiles[group, half][:], in_=block.rearrange("(p t) n -> p t n", t=SLOTS))
 
-        def load_f(half, kp):
-            f_raw[half, kp] = load_rows(F, kp, half)
+        def load_c_scales():
+            for q in range(QUADRANTS):
+                nc.sync.dma_start(
+                    out=c_scales_raw[32 * q : 32 * q + 4].bitcast(I32),
+                    in_=C_scales[:, span(q, 4), :].rearrange("g r n -> r g n").bitcast(I32),
+                )
 
-        def load_b_old(half, g):
-            b_old[half, g] = load_rows(B_old, g, half)
 
-        def copy_on(on_vector, out, in_):
+        def copy(on_vector, out, in_):
             if on_vector:
                 nc.vector.tensor_copy(out=out, in_=in_)
             else:
                 nc.scalar.copy(out=out, in_=in_)
 
-        def interleave(on_vector, out, in_):
-            copy_on(on_vector, out.rearrange("p (c i) t -> p c t i", i=RUN), in_.rearrange("p t (c i) -> p c t i", i=RUN))
+        def walk_cols(by_column):
+            return by_column.rearrange("p (c i) t -> p c t i", i=RUN)
 
-        def quantize(src, name, bufs):
-            width = src.shape[1]
-            codes = work.tile([P, width], U32, name=name + "_codes", bufs=bufs, align_bytes=64)
-            scales = work.tile([P, width], U8, name=name + "_scales", bufs=bufs, align_bytes=64)
-            nc.vector.quantize_mx(out=codes[:].bitcast(FP8X4), scales=scales[:], in_=src.rearrange("p n t -> p (n t)"))
+        def walk_slots(by_slot):
+            return by_slot.rearrange("p t (c i) -> p c t i", i=RUN)
+
+        def wide_stage():
+            return work.tile([P, WIDE, SLOTS], BF16, name="wide_stage", bufs=WIDE_STAGES, align_bytes=64)
+
+        def narrow_stage():
+            return work.tile([P, CHUNK, SLOTS], BF16, name="narrow_stage", bufs=NARROW_STAGES, align_bytes=64)
+
+        def mx_tiles(shape, name, bufs):
+            codes = work.tile(shape, U32, name=name + "_codes", bufs=bufs, align_bytes=64)
+            scales = work.tile(shape, U8, name=name + "_scales", bufs=bufs, align_bytes=64)
             return codes, scales
 
-        def interleave_z(kp, g, split):
-            z_il[kp, g] = work.tile([P, GROUP, PACK], BF16, name="z_il", bufs=5, align_bytes=64)
-            out = z_il[kp, g][:].rearrange("p (t m i) j -> p t m j i", t=PACK, i=2)
-            in_ = z_raw[kp, g][:].rearrange("p j (m i t) -> p t m j i", t=PACK, i=2)
-            if split < PACK:
-                nc.scalar.copy(out=out[:, split:], in_=in_[:, split:])
-            if split:
-                nc.vector.tensor_copy(out=out[:, :split], in_=in_[:, :split])
+        def quantize(codes, scales, by_column):
+            nc.vector.quantize_mx(out=codes.bitcast(FP8X4), scales=scales, in_=by_column.rearrange("p n t -> p (n t)"))
 
-        def quantize_z(kp, g):
-            z_mx[kp, g] = quantize(z_il[kp, g][:], "z", 12)
+        def lay_out_z(kp, g, share):
+            z_cols[kp, g] = wide_stage()
+            out = z_cols[kp, g][:].rearrange("p (s m i) t -> p s m t i", s=SLOTS, i=Z_RUN)
+            in_ = z_rows[kp, g][:].rearrange("p t (m i s) -> p s m t i", s=SLOTS, i=Z_RUN)
+            nc.scalar.copy(out=out[:, share:], in_=in_[:, share:])
+            if share:
+                nc.vector.tensor_copy(out=out[:, :share], in_=in_[:, :share])
 
-        def interleave_f(c, kp, share=0):
-            f_il[c, kp] = work.tile([P, CHUNK, PACK], BF16, name="f_il", bufs=6, align_bytes=64)
-            first = c * CHUNK % LOAD_COLS
-            interleave(share, f_il[c, kp][:], f_raw[c * CHUNK // LOAD_COLS, kp][:, :, first : first + CHUNK])
+        def lay_out_f_wide(kp, share):
+            f_cols[0, kp] = wide_stage()
+            split = share * WIDE // 4
+            nc.scalar.copy(out=walk_cols(f_cols[0, kp][:, split:]), in_=walk_slots(f_rows[kp, 0][:, :, split:]))
+            if share:
+                nc.vector.tensor_copy(out=walk_cols(f_cols[0, kp][:, :split]), in_=walk_slots(f_rows[kp, 0][:, :, :split]))
+
+        def quantize_f_wide(kp):
+            f_mx[0, kp] = mx_tiles([P, WIDE], "streamed", PASSES * (GROUPS + 1))
+            quantize(f_mx[0, kp][0][:], f_mx[0, kp][1][:], f_cols[0, kp][:])
+
+        def lay_out_f(c, kp):
+            f_cols[c, kp] = narrow_stage()
+            nc.scalar.copy(out=walk_cols(f_cols[c, kp][:]), in_=walk_slots(f_rows[kp, 1][:, :, span(c % 2, CHUNK)]))
 
         def quantize_f(c, kp):
-            f_mx[c, kp] = quantize(f_il[c, kp][:], "f", 8)
+            f_mx[c, kp] = mx_tiles([P, CHUNK], "f", 2 * PASSES)
+            quantize(f_mx[c, kp][0][:], f_mx[c, kp][1][:], f_cols[c, kp][:])
 
-        def interleave_f_head(kp, share):
-            f_il[0, kp] = work.tile([P, LOAD_COLS, PACK], BF16, name="z_il", bufs=5, align_bytes=64)
-            split = share * 128
-            if share < 4:
-                interleave(False, f_il[0, kp][:, split:], f_raw[0, kp][:, :, split:])
-            if split:
-                interleave(True, f_il[0, kp][:, :split], f_raw[0, kp][:, :, :split])
+        def deal(out, in_):
+            nc.vector.tensor_copy(
+                out=out.rearrange("p k (g s m) -> p (k g) s m", g=GROUPS, s=SLOTS),
+                in_=in_.rearrange("p k (g m s) -> p (k g) s m", g=GROUPS, s=SLOTS),
+            )
 
-        def quantize_f_head(kp):
-            f_mx[0, kp] = quantize(f_il[0, kp][:], "z", 12)
-
-        def mx_pass(out, lhs, lhs_scale, rhs, cols, start, stop):
-            nc.tensor.matmul_mx(out=out, lhsT=lhs, lhsT_scale=lhs_scale, rhs=rhs[0][:, cols].bitcast(FP8X4), rhs_scale=rhs[1][:, cols], start=start, stop=stop)
 
         def z_pass(out, c, kp, g, t):
-            cols = slice(t * P, (t + 1) * P)
-            mx_pass(out, z_mx[kp, g][0][:, cols].bitcast(FP8X4), z_mx[kp, g][1][:, cols], f_mx[c, kp], slice(0, out.shape[1]), kp == 0, kp == SUB_PASSES - 1)
+            codes, scales = z_mx[kp, g]
+            nc.tensor.matmul_mx(
+                out=out, lhsT=codes[:, span(t, P)].bitcast(FP8X4), lhsT_scale=scales[:, span(t, P)],
+                rhs=f_mx[c, kp][0][:].bitcast(FP8X4), rhs_scale=f_mx[c, kp][1][:],
+                start=kp == 0, stop=kp == PASSES - 1,
+            )
 
-        def c_group(out, g, t, rhs, first):
-            col = g * GROUP + t * P
-            for kg in range(GROUPS):
-                mx_pass(out, c_words[:, kg, 2 * col : 2 * (col + P)].bitcast(FP4X4), c_scales[:, kg, col : col + P],
-                        rhs, slice(first(kg), first(kg) + HALF), kg == 0, kg == GROUPS - 1)
-
-        def moments(c, b):
-            banks[1, c, b] = psum.tile([P, 2, CHUNK], F32, name="bank")
-            for i in range(2):
-                for kp in range(SUB_PASSES):
-                    z_pass(banks[1, c, b][:, i, :], c, kp, b // 2, 2 * (b % 2) + i)
-
-        def moments_head(kp, g):
-            for t in range(PACK):
+        def quantize_z_and_multiply(kp, g):
+            z_mx[kp, g] = mx_tiles([P, WIDE], "streamed", PASSES * (GROUPS + 1))
+            quantize(z_mx[kp, g][0][:], z_mx[kp, g][1][:], z_cols[kp, g][:])
+            for t in range(SLOTS):
                 if kp == 0:
-                    banks[0, g, t] = psum.tile([P, LOAD_COLS], F32, name="bank")
-                z_pass(banks[0, g, t][:], 0, kp, g, t)
+                    banks["wide", g, t] = psum.tile([P, WIDE], F32, name="bank")
+                z_pass(banks["wide", g, t][:], 0, kp, g, t)
 
-        def add_old_head(g, t):
-            nc.vector.tensor_tensor(out=b_all[:, g, t, :LOAD_COLS], in0=banks[0, g, t][:], in1=b_old[0, g][:, t, :], op=ALU.add)
+        def add_old_wide(g, t, cols):
+            nc.vector.tensor_tensor(
+                out=b_f32[:, g, t, cols], in0=banks["wide", g, t][:, cols], in1=b_old[g, 0][:, t, cols], op=ALU.add
+            )
 
-        def add_old_part(c, t):
-            cols = slice(c * CHUNK, (c + 1) * CHUNK)
-            nc.vector.tensor_tensor(out=b_all[:, 1, t, cols], in0=banks[0, 1, t][:, cols], in1=b_old[0, 1][:, t, cols], op=ALU.add)
+        def first_product(c, b):
+            banks["first", c, b] = psum.tile([P, 2, CHUNK], F32, name="bank")
+            for i in range(2):
+                for kp in range(PASSES):
+                    z_pass(banks["first", c, b][:, i, :], c, kp, b // 2, 2 * (b % 2) + i)
 
         def add_old(c, b):
-            first = c * CHUNK % LOAD_COLS
-            slots = slice(2 * (b % 2), 2 * (b % 2) + 2)
-            nc.vector.tensor_tensor(out=b_f32[c][:, b // 2, slots, :], in0=banks[1, c, b][:],
-                                    in1=b_old[c * CHUNK // LOAD_COLS, b // 2][:, slots, first : first + CHUNK], op=ALU.add)
+            slots = span(b % 2, 2)
+            nc.vector.tensor_tensor(
+                out=b_f32[:, b // 2, slots, span(c, CHUNK)], in0=banks["first", c, b][:],
+                in1=b_old[b // 2, 1][:, slots, span(c % 2, CHUNK)], op=ALU.add,
+            )
 
         def round_b(c, g, on_vector=False):
-            if c not in b_il:
-                b_il[c] = work.tile([P, GROUPS * CHUNK, PACK], BF16, name="z_il", bufs=5, align_bytes=64)
-            interleave(on_vector, b_il[c][:, g * CHUNK : (g + 1) * CHUNK, :], b_f32[c][:, g])
+            if g == 0:
+                b_cols[c] = wide_stage()
+            copy(on_vector, walk_cols(b_cols[c][:, span(g, CHUNK), :]), walk_slots(b_f32[:, g, :, span(c, CHUNK)]))
 
         def quantize_b(c):
-            b_mx[c] = quantize(b_il[c][:], "b", 2)
+            b_mx[c] = mx_tiles([P, GROUPS * CHUNK], "b", 2)
+            quantize(b_mx[c][0][:], b_mx[c][1][:], b_cols[c][:])
 
-        def scale_b(pair, g, t):
-            if t == 0:
-                y_f32[pair, g] = work.tile([P, PACK, WIDE], F32, name="y_f32", bufs=4)
-            nc.scalar.activation(out=y_f32[pair, g][:, t, :], in_=b_all[:, g, t, pair * WIDE : (pair + 1) * WIDE], func=ACT.Copy,
-                                 scale=gain[:, g * PACK + t : g * PACK + t + 1])
+        def scale_b(pair, g):
+            y_f32[pair, g] = work.tile([P, SLOTS, WIDE], F32, name="y_f32", bufs=2 * GROUPS)
+            for t in range(SLOTS):
+                nc.scalar.activation(
+                    out=y_f32[pair, g][:, t, :], in_=b_f32[:, g, t, span(pair, WIDE)], func=ACT.Copy,
+                    scale=gain[:, span(g * SLOTS + t, 1)],
+                )
 
-        def first_step(c, b):
-            h, g = b // 2, b % 2
-            banks[2, c, b] = psum.tile([P, PACK, HALF], F32, name="bank")
-            for t in range(PACK):
-                c_group(banks[2, c, b][:, t, :], g, t, b_mx[c], lambda kg: kg * CHUNK + h * HALF)
+
+        def c_product(out, g, t, rhs_codes, rhs_scales):
+            col = g * SLOTS + t
+            for kg in range(GROUPS):
+                nc.tensor.matmul_mx(
+                    out=out, lhsT=c_words[:, kg, span(col, 2 * P)].bitcast(FP4X4), lhsT_scale=c_scales[:, kg, span(col, P)],
+                    rhs=rhs_codes[kg].bitcast(FP8X4), rhs_scale=rhs_scales[kg], start=kg == 0, stop=kg == GROUPS - 1,
+                )
+
+        def second_product(c, b):
+            banks["second", c, b] = psum.tile([P, SLOTS, NARROW], F32, name="bank")
+            codes, scales = b_mx[c]
+            cols = [span(2 * kg + b // 2, NARROW) for kg in range(GROUPS)]
+            for t in range(SLOTS):
+                c_product(banks["second", c, b][:, t, :], b % 2, t, [codes[:, s] for s in cols], [scales[:, s] for s in cols])
 
         def subtract_h(c, b):
-            h, g = b // 2, b % 2
-            if c not in h_il:
-                h_il[c] = work.tile([P, GROUPS * CHUNK, PACK], BF16, name="z_il", bufs=5, align_bytes=64)
-            first = g * CHUNK + h * HALF
+            if b == 0:
+                h_cols[c] = wide_stage()
             nc.vector.tensor_tensor(
-                out=h_il[c][:, first : first + HALF, :].rearrange("p (c i) t -> p c t i", i=2),
-                in0=b_f32[c][:, g, :, h * HALF : (h + 1) * HALF].rearrange("p t (c i) -> p c t i", i=2),
-                in1=banks[2, c, b][:].rearrange("p t (c i) -> p c t i", i=2), op=ALU.subtract)
+                out=walk_cols(h_cols[c][:, span(2 * (b % 2) + b // 2, NARROW), :]),
+                in0=walk_slots(b_f32[:, b % 2, :, span(2 * c + b // 2, NARROW)]),
+                in1=walk_slots(banks["second", c, b][:]), op=ALU.subtract,
+            )
 
         def quantize_h(c):
             if c % 2 == 0:
-                codes = work.tile([P, GROUPS, WIDE], U32, name="h_codes", align_bytes=64)
-                scales = work.tile([P, GROUPS, WIDE], U8, name="h_scales", align_bytes=64)
-                h_mx[c // 2] = codes, scales
+                h_mx[c // 2] = mx_tiles([P, GROUPS, WIDE], "h", 2)
             codes, scales = h_mx[c // 2]
-            cols = slice(c % 2 * CHUNK, (c % 2 + 1) * CHUNK)
             for g in range(GROUPS):
-                nc.vector.quantize_mx(out=codes[:, g, cols].bitcast(FP8X4), scales=scales[:, g, cols],
-                                      in_=h_il[c][:, g * CHUNK : (g + 1) * CHUNK, :].rearrange("p n t -> p (n t)"))
+                quantize(codes[:, g, span(c % 2, CHUNK)], scales[:, g, span(c % 2, CHUNK)], h_cols[c][:, span(g, CHUNK), :])
 
-        def second_step(pair, g, t):
-            banks[3, pair, g, t] = psum.tile([P, WIDE], F32, name="bank")
-            col = g * GROUP + t * P
+        def third_product(pair, g, t):
+            banks["third", pair, g, t] = psum.tile([P, WIDE], F32, name="bank")
             codes, scales = h_mx[pair]
-            for kg in range(GROUPS):
-                nc.tensor.matmul_mx(out=banks[3, pair, g, t][:], lhsT=c_words[:, kg, 2 * col : 2 * (col + P)].bitcast(FP4X4),
-                                    lhsT_scale=c_scales[:, kg, col : col + P], rhs=codes[:, kg, :].bitcast(FP8X4),
-                                    rhs_scale=scales[:, kg, :], start=kg == 0, stop=kg == GROUPS - 1)
+            c_product(banks["third", pair, g, t][:], g, t, [codes[:, kg, :] for kg in range(GROUPS)],
+                      [scales[:, kg, :] for kg in range(GROUPS)])
 
         def finish_y(pair, g, t):
-            nc.vector.scalar_tensor_tensor(out=y_f32[pair, g][:, t, :], in0=banks[3, pair, g, t][:],
-                                           scalar=minus_gain[:, g * PACK + t : g * PACK + t + 1], in1=y_f32[pair, g][:, t, :],
-                                           op0=ALU.mult, op1=ALU.add)
-
-        def store_y(pair, g, t):
-            dst = out_0[g * GROUP : (g + 1) * GROUP, pair * WIDE : (pair + 1) * WIDE]
-            nc.sync.dma_start(out=dst.rearrange("(p t) m -> p t m", t=PACK)[:, t, :], in_=y_f32[pair, g][:, t, :])
+            y = y_f32[pair, g][:, t, :]
+            nc.vector.scalar_tensor_tensor(
+                out=y, in0=banks["third", pair, g, t][:], scalar=minus_gain[:, span(g * SLOTS + t, 1)], in1=y,
+                op0=ALU.mult, op1=ALU.add,
+            )
+            dst = out_0[span(g, GROUP), span(pair, WIDE)].rearrange("(p t) m -> p t m", t=SLOTS)
+            nc.sync.dma_start(out=dst[:, t, :], in_=y)
 
         def round_y(c, g, on_vector=False):
-            y_il[c, g] = work.tile([P, CHUNK, PACK], BF16, name="f_il", bufs=6, align_bytes=64)
-            interleave(on_vector, y_il[c, g][:], y_f32[c // 2, g][:, :, c % 2 * CHUNK : (c % 2 + 1) * CHUNK])
+            y_cols[c, g] = narrow_stage()
+            copy(on_vector, walk_cols(y_cols[c, g][:]), walk_slots(y_f32[c // 2, g][:, :, span(c % 2, CHUNK)]))
 
         def quantize_y(c, g):
-            cols = slice(c * CHUNK, (c + 1) * CHUNK)
             codes = work.tile([P, CHUNK], U32, name="y_codes", bufs=4, align_bytes=64)
-            nc.vector.quantize_mx(out=codes[:].bitcast(FP8X4), scales=y_scales[:, g, cols], in_=y_il[c, g][:].rearrange("p n t -> p (n t)"))
-            y_codes[c, g] = codes
+            quantize(codes[:], y_scales[:, g, span(c, CHUNK)], y_cols[c, g][:])
+            dst = out_1[g, :, span(c, CHUNK), :].rearrange("p m t -> p (m t)")
+            nc.sync.dma_start(out=dst.bitcast(I32), in_=codes[:].bitcast(I32))
 
-        def store_codes(c, g):
-            cols = slice(c * CHUNK, (c + 1) * CHUNK)
-            nc.sync.dma_start(out=out_1[g, :, cols, :].rearrange("p m t -> p (m t)").bitcast(I32), in_=y_codes[c, g][:].bitcast(I32))
+        def each_bank(step, *key):
+            for b in range(BANKS):
+                step(*key, b)
 
-        def load_c_words():
-            nc.sync.dma_start(out=c_words_raw[:].bitcast(I32), in_=C_words.rearrange("g p b -> p g b").bitcast(I32))
-
-        def load_c_scales():
-            for q in range(4):
-                nc.sync.dma_start(out=c_scales_raw[32 * q : 32 * q + 4].bitcast(I32),
-                                  in_=C_scales[:, 4 * q : 4 * q + 4, :].rearrange("g r n -> r g n").bitcast(I32))
-
-        def load_gain():
-            nc.sync.dma_start(out=gain_raw[:], in_=inv_sd.rearrange("(g p t) -> p g t", g=GROUPS, t=PACK))
-
-        def deal_c_words():
-            nc.vector.tensor_copy(
-                out=c_words[:].bitcast(U16).rearrange("p k (g t m) -> p (k g) t m", g=GROUPS, t=PACK),
-                in_=c_words_raw[:].bitcast(U16).rearrange("p k (g m t) -> p (k g) t m", g=GROUPS, t=PACK))
-
-        def deal_c_scales():
-            nc.vector.tensor_copy(
-                out=c_scales[:].rearrange("p k (g t m) -> p (k g) t m", g=GROUPS, t=PACK),
-                in_=c_scales_raw[:].rearrange("p k (g m t) -> p (k g) t m", g=GROUPS, t=PACK))
-
-        def gains():
-            nc.vector.tensor_copy(out=gain[:], in_=gain_raw[:].rearrange("p g t -> p (g t)"))
-            nc.vector.tensor_scalar(out=minus_gain[:], in0=gain_raw[:].rearrange("p g t -> p (g t)"), scalar1=-1.0, scalar2=None, op0=ALU.mult)
+        def weave(step, key, between):
+            for b in range(BANKS):
+                step(*key, b)
+                for call in between[b]:
+                    call[0](*call[1:])
 
         nc.vector.memset(c_scales_raw[:].rearrange("p g n -> p (g n)").bitcast(I32), 0)
+        for kp in range(PASSES):
+            if kp == 2:
+                load_c_scales()
+            load_rows(f_rows, F, kp, 0)
+            load_rows(z_rows, Z, kp, 0)
+        for kp in range(PASSES):
+            load_rows(z_rows, Z, kp, 1)
+        load_rows(b_old, B_old, 0, 0)
+        nc.sync.dma_start(out=c_words_raw[:].bitcast(I32), in_=C_words.rearrange("g p b -> p g b").bitcast(I32))
+        load_rows(b_old, B_old, 1, 0)
+        nc.sync.dma_start(out=gain_raw[:], in_=inv_sd.rearrange("(g p t) -> p g t", g=GROUPS, t=SLOTS))
+        late_loads = [(f_rows, F, kp, 1) for kp in range(PASSES)] + [(b_old, B_old, g, 1) for g in range(GROUPS)]
+        load_rows(*late_loads[0])
 
-        def store_scales(first=0, last=CHUNKS):
-            cols = slice(first * CHUNK, last * CHUNK)
-            for q in range(4):
-                nc.scalar.dma_start(out=out_2[:, 4 * q : 4 * q + 4, cols].rearrange("g r n -> r g n").bitcast(I32),
-                                  in_=y_scales[32 * q : 32 * q + 4, :, cols].bitcast(I32))
+        for kp in range(PASSES):
+            lay_out_f_wide(kp, 0 if kp == 2 else EVEN_SHARE)
+            if 2 * kp + 1 < len(late_loads):
+                load_rows(*late_loads[2 * kp + 1])
+            if kp:
+                quantize_z_and_multiply(kp - 1, 0)
+            if kp == 2:
+                deal(c_scales[:], c_scales_raw[:])
+            lay_out_z(kp, 0, EVEN_SHARE)
+            if 2 * kp + 2 < len(late_loads):
+                load_rows(*late_loads[2 * kp + 2])
+            quantize_f_wide(kp)
+        streamed = [(PASSES - 1, 0)] + [(kp, 1) for kp in range(PASSES)]
+        for before, now in zip(streamed, streamed[1:]):
+            lay_out_z(*now, 0 if now == streamed[-1] else EVEN_SHARE)
+            quantize_z_and_multiply(*before)
+        weave(lambda t: add_old_wide(0, t, span(0, WIDE)), (), [[], [], [(quantize_z_and_multiply, *streamed[-1])], []])
+        round_b(0, 0)
+        round_b(1, 0)
+        deal(c_words[:].bitcast(U16), c_words_raw[:].bitcast(U16))
 
-        steps = {
-            "LCW": load_c_words, "LCS": load_c_scales, "LG": load_gain, "CW": deal_c_words, "CS": deal_c_scales, "G": gains,
-            "LZ": load_z, "LF": load_f, "LB": load_b_old, "ZI": interleave_z, "QZ": quantize_z, "FH": interleave_f_head, "QFH": quantize_f_head,
-            "M": moments_head, "FI": interleave_f, "QF": quantize_f, "SC": store_scales, "Sa": moments, "Sb": first_step, "Sc": second_step,
-            "AH": add_old_head, "AG": add_old_part, "A": add_old, "BI": round_b, "QB": quantize_b, "BS": scale_b, "H": subtract_h, "QH": quantize_h,
-            "Y": finish_y, "YI": round_y, "QY": quantize_y, "SY": store_y, "SQ": store_codes,
-        }
-        steps["LF"](0, 0)
-        steps["LZ"](0, 0)
-        steps["LF"](0, 1)
-        steps["LZ"](1, 0)
-        steps["LCS"]()
-        steps["LF"](0, 2)
-        steps["LZ"](2, 0)
-        steps["LF"](0, 3)
-        steps["LZ"](3, 0)
-        steps["LZ"](0, 1)
-        steps["LZ"](1, 1)
-        steps["LZ"](2, 1)
-        steps["LZ"](3, 1)
-        steps["LB"](0, 0)
-        steps["LCW"]()
-        steps["LB"](0, 1)
-        steps["LG"]()
-        steps["LF"](1, 0)
-        steps["FH"](0, 2)
-        steps["LF"](1, 1)
-        steps["ZI"](0, 0, 2)
-        steps["LF"](1, 2)
-        steps["QFH"](0)
-        steps["FH"](1, 2)
-        steps["LF"](1, 3)
-        steps["QZ"](0, 0)
-        steps["M"](0, 0)
-        steps["ZI"](1, 0, 2)
-        steps["LB"](1, 0)
-        steps["QFH"](1)
-        steps["FH"](2, 0)
-        steps["LB"](1, 1)
-        steps["QZ"](1, 0)
-        steps["M"](1, 0)
-        steps["CS"]()
-        steps["ZI"](2, 0, 2)
-        steps["QFH"](2)
-        steps["FH"](3, 2)
-        steps["QZ"](2, 0)
-        steps["M"](2, 0)
-        steps["ZI"](3, 0, 2)
-        steps["QFH"](3)
-        steps["ZI"](0, 1, 2)
-        steps["QZ"](3, 0)
-        steps["M"](3, 0)
-        steps["ZI"](1, 1, 2)
-        steps["QZ"](0, 1)
-        steps["M"](0, 1)
-        steps["ZI"](2, 1, 2)
-        steps["QZ"](1, 1)
-        steps["M"](1, 1)
-        steps["ZI"](3, 1, 0)
-        steps["QZ"](2, 1)
-        steps["M"](2, 1)
-        steps["AH"](0, 0)
-        steps["AH"](0, 1)
-        steps["AH"](0, 2)
-        steps["QZ"](3, 1)
-        steps["M"](3, 1)
-        steps["AH"](0, 3)
-        steps["BI"](0, 0)
-        steps["BI"](1, 0)
-        steps["CW"]()
-        steps["AG"](0, 0)
-        steps["AG"](0, 1)
-        steps["AG"](0, 2)
-        steps["AG"](0, 3)
-        steps["BI"](0, 1, 4)
-        steps["AG"](1, 0)
-        steps["AG"](1, 1)
-        steps["QB"](0)
-        steps["Sb"](0, 0)
-        steps["Sb"](0, 1)
-        steps["Sb"](0, 2)
-        steps["Sb"](0, 3)
-        steps["AG"](1, 2)
-        steps["AG"](1, 3)
-        steps["FI"](2, 0)
-        steps["FI"](2, 1)
-        steps["FI"](2, 2)
-        steps["FI"](2, 3)
-        steps["FI"](3, 0)
-        steps["FI"](3, 1)
-        steps["G"]()
-        steps["BI"](1, 1, 4)
-        steps["QF"](2, 0)
-        steps["QF"](2, 1)
-        steps["FI"](3, 2)
-        steps["FI"](3, 3)
-        steps["QB"](1)
-        steps["Sb"](1, 0)
-        steps["Sb"](1, 1)
-        steps["Sb"](1, 2)
-        steps["Sb"](1, 3)
-        steps["H"](0, 0)
-        steps["H"](0, 1)
-        steps["QF"](2, 2)
-        steps["H"](0, 2)
-        steps["H"](0, 3)
-        steps["QF"](2, 3)
-        steps["Sa"](2, 0)
-        steps["Sa"](2, 1)
-        steps["Sa"](2, 2)
-        steps["Sa"](2, 3)
-        steps["H"](1, 0)
-        steps["QH"](0)
-        steps["H"](1, 1)
-        steps["QF"](3, 0)
-        steps["H"](1, 2)
-        steps["QF"](3, 1)
-        steps["H"](1, 3)
-        steps["QF"](3, 2)
-        steps["A"](2, 0)
-        steps["QF"](3, 3)
-        steps["Sa"](3, 0)
-        steps["QH"](1)
-        steps["A"](2, 1)
-        steps["Sa"](3, 1)
-        steps["BS"](0, 0, 0)
-        steps["BS"](0, 0, 1)
-        steps["BS"](0, 0, 2)
-        steps["BS"](0, 0, 3)
-        steps["A"](2, 2)
-        steps["BI"](2, 0)
-        steps["Sa"](3, 2)
-        steps["A"](2, 3)
-        steps["Sa"](3, 3)
-        steps["BI"](2, 1)
-        steps["A"](3, 0)
-        steps["A"](3, 1)
-        steps["Sc"](0, 0, 0)
-        steps["Sc"](0, 0, 1)
-        steps["QB"](2)
-        steps["BI"](3, 0)
-        steps["A"](3, 2)
-        steps["Sc"](0, 0, 2)
-        steps["A"](3, 3)
-        steps["Sc"](0, 0, 3)
-        steps["BI"](3, 1)
-        steps["BS"](0, 1, 0)
-        steps["BS"](0, 1, 1)
-        steps["BS"](0, 1, 2)
-        steps["BS"](0, 1, 3)
-        steps["Sb"](2, 0)
-        steps["Sb"](2, 1)
-        steps["Sb"](2, 2)
-        steps["Sb"](2, 3)
-        steps["Y"](0, 0, 0)
-        steps["SY"](0, 0, 0)
-        steps["Y"](0, 0, 1)
-        steps["SY"](0, 0, 1)
-        steps["Y"](0, 0, 2)
-        steps["SY"](0, 0, 2)
-        steps["Y"](0, 0, 3)
-        steps["SY"](0, 0, 3)
-        steps["YI"](0, 0)
-        steps["YI"](1, 0)
-        steps["QB"](3)
-        steps["Sb"](3, 0)
-        steps["Sb"](3, 1)
-        steps["Sb"](3, 2)
-        steps["Sb"](3, 3)
-        steps["BS"](1, 0, 0)
-        steps["BS"](1, 0, 1)
-        steps["BS"](1, 0, 2)
-        steps["BS"](1, 0, 3)
-        steps["BS"](1, 1, 0)
-        steps["BS"](1, 1, 1)
-        steps["BS"](1, 1, 2)
-        steps["BS"](1, 1, 3)
-        steps["H"](2, 0)
-        steps["H"](2, 1)
-        steps["H"](2, 2)
-        steps["H"](2, 3)
-        steps["QY"](0, 0)
-        steps["SQ"](0, 0)
-        steps["Sc"](0, 1, 0)
-        steps["Sc"](0, 1, 1)
-        steps["Sc"](0, 1, 2)
-        steps["Sc"](0, 1, 3)
-        steps["H"](3, 0)
-        steps["QH"](2)
-        steps["H"](3, 1)
-        steps["QY"](1, 0)
-        steps["SQ"](1, 0)
-        steps["H"](3, 2)
-        steps["H"](3, 3)
-        steps["Y"](0, 1, 0)
-        steps["SY"](0, 1, 0)
-        steps["QH"](3)
-        steps["Sc"](1, 0, 0)
-        steps["Sc"](1, 0, 1)
-        steps["Sc"](1, 0, 2)
-        steps["Sc"](1, 0, 3)
-        steps["Y"](0, 1, 1)
-        steps["SY"](0, 1, 1)
-        steps["Y"](0, 1, 2)
-        steps["SY"](0, 1, 2)
-        steps["Y"](0, 1, 3)
-        steps["SY"](0, 1, 3)
-        steps["Sc"](1, 1, 0)
-        steps["Sc"](1, 1, 1)
-        steps["Sc"](1, 1, 2)
-        steps["Sc"](1, 1, 3)
-        steps["YI"](0, 1)
-        steps["YI"](1, 1)
-        steps["Y"](1, 0, 0)
-        steps["SY"](1, 0, 0)
-        steps["Y"](1, 0, 1)
-        steps["SY"](1, 0, 1)
-        steps["Y"](1, 0, 2)
-        steps["SY"](1, 0, 2)
-        steps["Y"](1, 0, 3)
-        steps["SY"](1, 0, 3)
-        steps["YI"](2, 0)
-        steps["YI"](3, 0)
-        steps["QY"](0, 1)
-        steps["SQ"](0, 1)
-        steps["Y"](1, 1, 0)
-        steps["SY"](1, 1, 0)
-        steps["Y"](1, 1, 1)
-        steps["SY"](1, 1, 1)
-        steps["QY"](1, 1)
-        steps["SQ"](1, 1)
-        steps["Y"](1, 1, 2)
-        steps["SY"](1, 1, 2)
-        steps["Y"](1, 1, 3)
-        steps["SY"](1, 1, 3)
-        steps["QY"](2, 0)
-        steps["SQ"](2, 0)
-        steps["YI"](2, 1)
-        steps["YI"](3, 1, 4)
-        steps["QY"](3, 0)
-        steps["SQ"](3, 0)
-        steps["QY"](3, 1)
-        steps["SQ"](3, 1)
-        steps["QY"](2, 1)
-        steps["SQ"](2, 1)
-        steps["SC"]()
+        each_bank(lambda t: add_old_wide(1, t, span(0, CHUNK)))
+        round_b(0, 1, on_vector=True)
+        weave(lambda t: add_old_wide(1, t, span(1, CHUNK)), (), [[], [(quantize_b, 0), (each_bank, second_product, 0)], [], []])
+        each_bank(lay_out_f, 2)
+        lay_out_f(3, 0)
+        lay_out_f(3, 1)
+        gain_flat = gain_raw[:].rearrange("p g t -> p (g t)")
+        nc.vector.tensor_copy(out=gain[:], in_=gain_flat)
+        nc.vector.tensor_scalar(out=minus_gain[:], in0=gain_flat, scalar1=-1.0, scalar2=None, op0=ALU.mult)
+        round_b(1, 1, on_vector=True)
+        quantize_f(2, 0)
+        quantize_f(2, 1)
+        lay_out_f(3, 2)
+        lay_out_f(3, 3)
+        quantize_b(1)
+        each_bank(second_product, 1)
+
+        weave(subtract_h, (0,), [[], [(quantize_f, 2, 2)], [], [(quantize_f, 2, 3), (each_bank, first_product, 2)]])
+        weave(subtract_h, (1,), [[(quantize_h, 0)], [(quantize_f, 3, 0)], [(quantize_f, 3, 1)], [(quantize_f, 3, 2)]])
+        weave(add_old, (2,), [
+            [(quantize_f, 3, 3), (first_product, 3, 0), (quantize_h, 1)],
+            [(first_product, 3, 1), (scale_b, 0, 0), (round_b, 2, 0)],
+            [(first_product, 3, 2)],
+            [(first_product, 3, 3), (round_b, 2, 1)],
+        ])
+        weave(add_old, (3,), [
+            [],
+            [(quantize_b, 2), (round_b, 3, 0)],
+            [],
+            [(each_bank, third_product, 0, 0), (round_b, 3, 1), (scale_b, 0, 1), (each_bank, second_product, 2)],
+        ])
+        each_bank(finish_y, 0, 0)
+        round_y(0, 0)
+        round_y(1, 0)
+        quantize_b(3)
+        each_bank(second_product, 3)
+        scale_b(1, 0)
+        scale_b(1, 1)
+        each_bank(subtract_h, 2)
+        quantize_y(0, 0)
+        each_bank(third_product, 0, 1)
+        weave(subtract_h, (3,), [[(quantize_h, 2)], [(quantize_y, 1, 0)], [], []])
+        weave(finish_y, (0, 1), [[(quantize_h, 3), (each_bank, third_product, 1, 0)], [], [], []])
+        each_bank(third_product, 1, 1)
+        round_y(0, 1)
+        round_y(1, 1)
+        each_bank(finish_y, 1, 0)
+        round_y(2, 0)
+        round_y(3, 0)
+        quantize_y(0, 1)
+        weave(finish_y, (1, 1), [[], [(quantize_y, 1, 1)], [], [(quantize_y, 2, 0)]])
+
+        round_y(2, 1)
+        round_y(3, 1, on_vector=True)
+        quantize_y(3, 0)
+        quantize_y(3, 1)
+        quantize_y(2, 1)
+        for q in range(QUADRANTS):
+            nc.scalar.dma_start(
+                out=out_2[:, span(q, 4), :].rearrange("g r n -> r g n").bitcast(I32),
+                in_=y_scales[32 * q : 32 * q + 4].bitcast(I32),
+            )

@@ -26,9 +26,10 @@ CHUNK = 256
 NARROW = 128
 BANKS = 4
 QUADRANTS = 4
+SCALE_ROWS = 4
 RUN = 4
 Z_RUN = 2
-EVEN_SHARE = 2
+VECTOR_SHARE = 2
 ROW_TILES = 15
 WIDE_STAGES = 5
 NARROW_STAGES = 6
@@ -52,7 +53,7 @@ def tile_datamodel_neumann_regression_k1_kernel(
         gain_raw = keep.tile([P, GROUPS, SLOTS], BF16, name="gain_raw")
         gain = keep.tile([P, GROUPS * SLOTS], F32, name="gain")
         minus_gain = keep.tile([P, GROUPS * SLOTS], F32, name="minus_gain")
-        y_scales = keep.tile([P, GROUPS, TEST], U8, name="y_scales", align_bytes=64)
+        y_scales = keep.tile([P, TEST], U8, name="y_scales", align_bytes=64)
         b_f32 = keep.tile([P, GROUPS, SLOTS, TEST], F32, name="b_f32")
 
         z_rows, f_rows, b_old = {}, {}, {}
@@ -72,8 +73,8 @@ def tile_datamodel_neumann_regression_k1_kernel(
         def load_c_scales():
             for q in range(QUADRANTS):
                 nc.sync.dma_start(
-                    out=c_scales_raw[32 * q : 32 * q + 4].bitcast(I32),
-                    in_=C_scales[:, span(q, 4), :].rearrange("g r n -> r g n").bitcast(I32),
+                    out=c_scales_raw[32 * q : 32 * q + SCALE_ROWS].bitcast(I32),
+                    in_=C_scales[:, span(q, SCALE_ROWS), :].rearrange("g r n -> r g n").bitcast(I32),
                 )
 
 
@@ -103,20 +104,18 @@ def tile_datamodel_neumann_regression_k1_kernel(
         def quantize(codes, scales, by_column):
             nc.vector.quantize_mx(out=codes.bitcast(FP8X4), scales=scales, in_=by_column.rearrange("p n t -> p (n t)"))
 
-        def lay_out_z(kp, g, share):
+        def lay_out_z(kp, g):
             z_cols[kp, g] = wide_stage()
             out = z_cols[kp, g][:].rearrange("p (s m i) t -> p s m t i", s=SLOTS, i=Z_RUN)
             in_ = z_rows[kp, g][:].rearrange("p t (m i s) -> p s m t i", s=SLOTS, i=Z_RUN)
-            nc.scalar.copy(out=out[:, share:], in_=in_[:, share:])
-            if share:
-                nc.vector.tensor_copy(out=out[:, :share], in_=in_[:, :share])
+            nc.scalar.copy(out=out[:, VECTOR_SHARE:], in_=in_[:, VECTOR_SHARE:])
+            nc.vector.tensor_copy(out=out[:, :VECTOR_SHARE], in_=in_[:, :VECTOR_SHARE])
 
-        def lay_out_f_wide(kp, share):
+        def lay_out_f_wide(kp):
             f_cols[0, kp] = wide_stage()
-            split = share * WIDE // 4
+            split = VECTOR_SHARE * WIDE // 4
             nc.scalar.copy(out=walk_cols(f_cols[0, kp][:, split:]), in_=walk_slots(f_rows[kp, 0][:, :, split:]))
-            if share:
-                nc.vector.tensor_copy(out=walk_cols(f_cols[0, kp][:, :split]), in_=walk_slots(f_rows[kp, 0][:, :, :split]))
+            nc.vector.tensor_copy(out=walk_cols(f_cols[0, kp][:, :split]), in_=walk_slots(f_rows[kp, 0][:, :, :split]))
 
         def quantize_f_wide(kp):
             f_mx[0, kp] = mx_tiles([P, WIDE], "streamed", PASSES * (GROUPS + 1))
@@ -153,7 +152,7 @@ def tile_datamodel_neumann_regression_k1_kernel(
                     banks["wide", g, t] = psum.tile([P, WIDE], F32, name="bank")
                 z_pass(banks["wide", g, t][:], 0, kp, g, t)
 
-        def add_old_wide(g, t, cols):
+        def add_old_wide(g, cols, t):
             nc.vector.tensor_tensor(
                 out=b_f32[:, g, t, cols], in0=banks["wide", g, t][:, cols], in1=b_old[g, 0][:, t, cols], op=ALU.add
             )
@@ -240,8 +239,8 @@ def tile_datamodel_neumann_regression_k1_kernel(
             copy(on_vector, walk_cols(y_cols[c, g][:]), walk_slots(y_f32[c // 2, g][:, :, span(c % 2, CHUNK)]))
 
         def quantize_y(c, g):
-            codes = work.tile([P, CHUNK], U32, name="y_codes", bufs=4, align_bytes=64)
-            quantize(codes[:], y_scales[:, g, span(c, CHUNK)], y_cols[c, g][:])
+            codes = work.tile([P, CHUNK], U32, name="y_codes", bufs=TEST // CHUNK * GROUPS, align_bytes=64)
+            quantize(codes[:], y_scales[SCALE_ROWS * g :, span(c, CHUNK)], y_cols[c, g][:])
             dst = out_1[g, :, span(c, CHUNK), :].rearrange("p m t -> p (m t)")
             nc.sync.dma_start(out=dst.bitcast(I32), in_=codes[:].bitcast(I32))
 
@@ -257,58 +256,66 @@ def tile_datamodel_neumann_regression_k1_kernel(
 
         nc.vector.memset(c_scales_raw[:].rearrange("p g n -> p (g n)").bitcast(I32), 0)
         for kp in range(PASSES):
-            if kp == 2:
-                load_c_scales()
             load_rows(f_rows, F, kp, 0)
+            if kp == 0:
+                load_c_scales()
             load_rows(z_rows, Z, kp, 0)
-        for kp in range(PASSES):
+        last = PASSES - 1
+        for kp in range(last):
             load_rows(z_rows, Z, kp, 1)
         load_rows(b_old, B_old, 0, 0)
-        nc.sync.dma_start(out=c_words_raw[:].bitcast(I32), in_=C_words.rearrange("g p b -> p g b").bitcast(I32))
+        load_rows(z_rows, Z, last, 1)
+        load_rows(f_rows, F, 0, 1)
         load_rows(b_old, B_old, 1, 0)
+        nc.sync.dma_start(out=c_words_raw[:].bitcast(I32), in_=C_words.rearrange("g p b -> p g b").bitcast(I32))
         nc.sync.dma_start(out=gain_raw[:], in_=inv_sd.rearrange("(g p t) -> p g t", g=GROUPS, t=SLOTS))
-        late_loads = [(f_rows, F, kp, 1) for kp in range(PASSES)] + [(b_old, B_old, g, 1) for g in range(GROUPS)]
-        load_rows(*late_loads[0])
+        late_loads = [(f_rows, F, kp, 1) for kp in range(1, PASSES)] + [(b_old, B_old, g, 1) for g in range(GROUPS)]
+
+        def late_load(index):
+            if index < len(late_loads):
+                load_rows(*late_loads[index])
 
         for kp in range(PASSES):
-            lay_out_f_wide(kp, 0 if kp == 2 else EVEN_SHARE)
-            if 2 * kp + 1 < len(late_loads):
-                load_rows(*late_loads[2 * kp + 1])
+            lay_out_f_wide(kp)
+            late_load(2 * kp)
             if kp:
                 quantize_z_and_multiply(kp - 1, 0)
-            if kp == 2:
+            else:
                 deal(c_scales[:], c_scales_raw[:])
-            lay_out_z(kp, 0, EVEN_SHARE)
-            if 2 * kp + 2 < len(late_loads):
-                load_rows(*late_loads[2 * kp + 2])
+            lay_out_z(kp, 0)
+            late_load(2 * kp + 1)
             quantize_f_wide(kp)
-        streamed = [(PASSES - 1, 0)] + [(kp, 1) for kp in range(PASSES)]
-        for before, now in zip(streamed, streamed[1:]):
-            lay_out_z(*now, 0 if now == streamed[-1] else EVEN_SHARE)
-            quantize_z_and_multiply(*before)
-        weave(lambda t: add_old_wide(0, t, span(0, WIDE)), (), [[], [], [(quantize_z_and_multiply, *streamed[-1])], []])
+        for kp in range(last):
+            lay_out_z(kp, 1)
+            quantize_z_and_multiply(*((kp - 1, 1) if kp else (last, 0)))
+        weave(add_old_wide, (0, span(0, WIDE)), [
+            [(quantize_z_and_multiply, last - 1, 1), (lay_out_z, last, 1)],
+            [(quantize_z_and_multiply, last, 1)],
+            [],
+            [],
+        ])
+
+        lay_out_f(2, 0)
         round_b(0, 0)
+        each_bank(add_old_wide, 1, span(0, CHUNK))
+        round_b(0, 1)
         round_b(1, 0)
         deal(c_words[:].bitcast(U16), c_words_raw[:].bitcast(U16))
-
-        each_bank(lambda t: add_old_wide(1, t, span(0, CHUNK)))
-        round_b(0, 1, on_vector=True)
-        weave(lambda t: add_old_wide(1, t, span(1, CHUNK)), (), [[], [(quantize_b, 0), (each_bank, second_product, 0)], [], []])
-        each_bank(lay_out_f, 2)
+        weave(add_old_wide, (1, span(1, CHUNK)), [[], [(quantize_b, 0), (each_bank, second_product, 0)], [], []])
+        for kp in range(1, PASSES):
+            lay_out_f(2, kp)
         lay_out_f(3, 0)
         lay_out_f(3, 1)
+        quantize_f(2, 0)
+        round_b(1, 1, on_vector=True)
         gain_flat = gain_raw[:].rearrange("p g t -> p (g t)")
         nc.vector.tensor_copy(out=gain[:], in_=gain_flat)
         nc.vector.tensor_scalar(out=minus_gain[:], in0=gain_flat, scalar1=-1.0, scalar2=None, op0=ALU.mult)
-        round_b(1, 1, on_vector=True)
-        quantize_f(2, 0)
-        quantize_f(2, 1)
-        lay_out_f(3, 2)
-        lay_out_f(3, 3)
         quantize_b(1)
         each_bank(second_product, 1)
+        lay_out_f(3, 2)
 
-        weave(subtract_h, (0,), [[], [(quantize_f, 2, 2)], [], [(quantize_f, 2, 3), (each_bank, first_product, 2)]])
+        weave(subtract_h, (0,), [[(quantize_f, 2, 1), (lay_out_f, 3, 3)], [(quantize_f, 2, 2)], [], [(quantize_f, 2, 3), (each_bank, first_product, 2)]])
         weave(subtract_h, (1,), [[(quantize_h, 0)], [(quantize_f, 3, 0)], [(quantize_f, 3, 1)], [(quantize_f, 3, 2)]])
         weave(add_old, (2,), [
             [(quantize_f, 3, 3), (first_product, 3, 0), (quantize_h, 1)],
@@ -350,6 +357,6 @@ def tile_datamodel_neumann_regression_k1_kernel(
         quantize_y(2, 1)
         for q in range(QUADRANTS):
             nc.scalar.dma_start(
-                out=out_2[:, span(q, 4), :].rearrange("g r n -> r g n").bitcast(I32),
-                in_=y_scales[32 * q : 32 * q + 4].bitcast(I32),
+                out=out_2[:, span(q, SCALE_ROWS), :].bitcast(I32),
+                in_=y_scales[32 * q : 32 * q + SCALE_ROWS * GROUPS].bitcast(I32),
             )

from contextlib import ExitStack

import concourse.mybir as mybir

SUBS, TRAIN, TEST = 2048, 1024, 1024
FLOPS = 2 * SUBS * TRAIN * TEST + 2 * 2 * TRAIN * TRAIN * TEST

F32 = mybir.dt.float32
BF16 = mybir.dt.bfloat16
I32 = mybir.dt.int32
U32 = mybir.dt.uint32
U16 = mybir.dt.uint16
U8 = mybir.dt.uint8
FP8X4 = mybir.dt.float8_e4m3fn_x4
FP4X4 = mybir.dt.float4_e2m1fn_x4
ALU = mybir.AluOpType
ACT = mybir.ActivationFunctionType

P = 128
SLOTS = 4
GROUP = P * SLOTS
PASSES = SUBS // GROUP
GROUPS = TRAIN // GROUP
WIDE = 512
CHUNK = 256
NARROW = 128
BANKS = 4
QUADRANTS = 4
SCALE_ROWS = 4
RUN = 4
Z_RUN = 2
VECTOR_SHARE = 2
ROW_TILES = 15
WIDE_STAGES = 5
NARROW_STAGES = 6


def tile_datamodel_neumann_regression_k1_kernel(
    tc, Z, F, B_old, C_words, C_scales, inv_sd, out_0, out_1, out_2
):
    nc = tc.nc
    with ExitStack() as ctx:
        keep = ctx.enter_context(tc.tile_pool(name="keep", bufs=1))
        rows = ctx.enter_context(tc.tile_pool(name="rows", bufs=ROW_TILES))
        work = ctx.enter_context(tc.tile_pool(name="work", bufs=2))
        psum = ctx.enter_context(tc.psum_pool(name="psum", bufs=8))
        ctx.enter_context(tc.manual_schedule())

        c_words_raw = keep.tile([P, GROUPS, 2 * TRAIN], U8, name="c_words_raw")
        c_scales_raw = keep.tile([P, GROUPS, TRAIN], U8, name="c_scales_raw")
        c_words = keep.tile([P, GROUPS, 2 * TRAIN], U8, name="c_words", align_bytes=64)
        c_scales = keep.tile([P, GROUPS, TRAIN], U8, name="c_scales", align_bytes=64)
        gain_raw = keep.tile([P, GROUPS, SLOTS], BF16, name="gain_raw")
        gain = keep.tile([P, GROUPS * SLOTS], F32, name="gain")
        minus_gain = keep.tile([P, GROUPS * SLOTS], F32, name="minus_gain")
        y_scales = keep.tile([P, TEST], U8, name="y_scales", align_bytes=64)
        b_f32 = keep.tile([P, GROUPS, SLOTS, TEST], F32, name="b_f32")

        z_rows, f_rows, b_old = {}, {}, {}
        z_cols, f_cols, b_cols, h_cols, y_cols = {}, {}, {}, {}, {}
        z_mx, f_mx, b_mx, h_mx = {}, {}, {}, {}
        y_f32, banks = {}, {}

        def span(index, width):
            return slice(index * width, (index + 1) * width)


        def load_rows(tiles, src, group, half):
            tiles[group, half] = rows.tile([P, SLOTS, WIDE], BF16, name="rows")
            block = src[span(group, GROUP), span(half, WIDE)]
            nc.sync.dma_start(out=tiles[group, half][:], in_=block.rearrange("(p t) n -> p t n", t=SLOTS))

        def load_c_scales():
            for q in range(QUADRANTS):
                nc.sync.dma_start(
                    out=c_scales_raw[32 * q : 32 * q + SCALE_ROWS].bitcast(I32),
                    in_=C_scales[:, span(q, SCALE_ROWS), :].rearrange("g r n -> r g n").bitcast(I32),
                )


        def copy(on_vector, out, in_):
            if on_vector:
                nc.vector.tensor_copy(out=out, in_=in_)
            else:
                nc.scalar.copy(out=out, in_=in_)

        def walk_cols(by_column):
            return by_column.rearrange("p (c i) t -> p c t i", i=RUN)

        def walk_slots(by_slot):
            return by_slot.rearrange("p t (c i) -> p c t i", i=RUN)

        def wide_stage():
            return work.tile([P, WIDE, SLOTS], BF16, name="wide_stage", bufs=WIDE_STAGES, align_bytes=64)

        def narrow_stage():
            return work.tile([P, CHUNK, SLOTS], BF16, name="narrow_stage", bufs=NARROW_STAGES, align_bytes=64)

        def mx_tiles(shape, name, bufs):
            codes = work.tile(shape, U32, name=name + "_codes", bufs=bufs, align_bytes=64)
            scales = work.tile(shape, U8, name=name + "_scales", bufs=bufs, align_bytes=64)
            return codes, scales

        def quantize(codes, scales, by_column):
            nc.vector.quantize_mx(out=codes.bitcast(FP8X4), scales=scales, in_=by_column.rearrange("p n t -> p (n t)"))

        def lay_out_z(kp, g):
            z_cols[kp, g] = wide_stage()
            out = z_cols[kp, g][:].rearrange("p (s m i) t -> p s m t i", s=SLOTS, i=Z_RUN)
            in_ = z_rows[kp, g][:].rearrange("p t (m i s) -> p s m t i", s=SLOTS, i=Z_RUN)
            nc.scalar.copy(out=out[:, VECTOR_SHARE:], in_=in_[:, VECTOR_SHARE:])
            nc.vector.tensor_copy(out=out[:, :VECTOR_SHARE], in_=in_[:, :VECTOR_SHARE])

        def lay_out_f_wide(kp):
            f_cols[0, kp] = wide_stage()
            split = VECTOR_SHARE * WIDE // 4
            nc.scalar.copy(out=walk_cols(f_cols[0, kp][:, split:]), in_=walk_slots(f_rows[kp, 0][:, :, split:]))
            nc.vector.tensor_copy(out=walk_cols(f_cols[0, kp][:, :split]), in_=walk_slots(f_rows[kp, 0][:, :, :split]))

        def quantize_f_wide(kp):
            f_mx[0, kp] = mx_tiles([P, WIDE], "streamed", PASSES * (GROUPS + 1))
            quantize(f_mx[0, kp][0][:], f_mx[0, kp][1][:], f_cols[0, kp][:])

        def lay_out_f(c, kp):
            f_cols[c, kp] = narrow_stage()
            nc.scalar.copy(out=walk_cols(f_cols[c, kp][:]), in_=walk_slots(f_rows[kp, 1][:, :, span(c % 2, CHUNK)]))

        def quantize_f(c, kp):
            f_mx[c, kp] = mx_tiles([P, CHUNK], "f", 2 * PASSES)
            quantize(f_mx[c, kp][0][:], f_mx[c, kp][1][:], f_cols[c, kp][:])

        def deal(out, in_):
            nc.vector.tensor_copy(
                out=out.rearrange("p k (g s m) -> p (k g) s m", g=GROUPS, s=SLOTS),
                in_=in_.rearrange("p k (g m s) -> p (k g) s m", g=GROUPS, s=SLOTS),
            )


        def z_pass(out, c, kp, g, t):
            codes, scales = z_mx[kp, g]
            nc.tensor.matmul_mx(
                out=out, lhsT=codes[:, span(t, P)].bitcast(FP8X4), lhsT_scale=scales[:, span(t, P)],
                rhs=f_mx[c, kp][0][:].bitcast(FP8X4), rhs_scale=f_mx[c, kp][1][:],
                start=kp == 0, stop=kp == PASSES - 1,
            )

        def quantize_z_and_multiply(kp, g):
            z_mx[kp, g] = mx_tiles([P, WIDE], "streamed", PASSES * (GROUPS + 1))
            quantize(z_mx[kp, g][0][:], z_mx[kp, g][1][:], z_cols[kp, g][:])
            for t in range(SLOTS):
                if kp == 0:
                    banks["wide", g, t] = psum.tile([P, WIDE], F32, name="bank")
                z_pass(banks["wide", g, t][:], 0, kp, g, t)

        def add_old_wide(g, cols, t):
            nc.vector.tensor_tensor(
                out=b_f32[:, g, t, cols], in0=banks["wide", g, t][:, cols], in1=b_old[g, 0][:, t, cols], op=ALU.add
            )

        def first_product(c, b):
            banks["first", c, b] = psum.tile([P, 2, CHUNK], F32, name="bank")
            for i in range(2):
                for kp in range(PASSES):
                    z_pass(banks["first", c, b][:, i, :], c, kp, b // 2, 2 * (b % 2) + i)

        def add_old(c, b):
            slots = span(b % 2, 2)
            nc.vector.tensor_tensor(
                out=b_f32[:, b // 2, slots, span(c, CHUNK)], in0=banks["first", c, b][:],
                in1=b_old[b // 2, 1][:, slots, span(c % 2, CHUNK)], op=ALU.add,
            )

        def round_b(c, g, on_vector=False):
            if g == 0:
                b_cols[c] = wide_stage()
            copy(on_vector, walk_cols(b_cols[c][:, span(g, CHUNK), :]), walk_slots(b_f32[:, g, :, span(c, CHUNK)]))

        def quantize_b(c):
            b_mx[c] = mx_tiles([P, GROUPS * CHUNK], "b", 2)
            quantize(b_mx[c][0][:], b_mx[c][1][:], b_cols[c][:])

        def scale_b(pair, g):
            y_f32[pair, g] = work.tile([P, SLOTS, WIDE], F32, name="y_f32", bufs=2 * GROUPS)
            for t in range(SLOTS):
                nc.scalar.activation(
                    out=y_f32[pair, g][:, t, :], in_=b_f32[:, g, t, span(pair, WIDE)], func=ACT.Copy,
                    scale=gain[:, span(g * SLOTS + t, 1)],
                )


        def c_product(out, g, t, rhs_codes, rhs_scales):
            col = g * SLOTS + t
            for kg in range(GROUPS):
                nc.tensor.matmul_mx(
                    out=out, lhsT=c_words[:, kg, span(col, 2 * P)].bitcast(FP4X4), lhsT_scale=c_scales[:, kg, span(col, P)],
                    rhs=rhs_codes[kg].bitcast(FP8X4), rhs_scale=rhs_scales[kg], start=kg == 0, stop=kg == GROUPS - 1,
                )

        def second_product(c, b):
            banks["second", c, b] = psum.tile([P, SLOTS, NARROW], F32, name="bank")
            codes, scales = b_mx[c]
            cols = [span(2 * kg + b // 2, NARROW) for kg in range(GROUPS)]
            for t in range(SLOTS):
                c_product(banks["second", c, b][:, t, :], b % 2, t, [codes[:, s] for s in cols], [scales[:, s] for s in cols])

        def subtract_h(c, b):
            if b == 0:
                h_cols[c] = wide_stage()
            nc.vector.tensor_tensor(
                out=walk_cols(h_cols[c][:, span(2 * (b % 2) + b // 2, NARROW), :]),
                in0=walk_slots(b_f32[:, b % 2, :, span(2 * c + b // 2, NARROW)]),
                in1=walk_slots(banks["second", c, b][:]), op=ALU.subtract,
            )

        def quantize_h(c):
            if c % 2 == 0:
                h_mx[c // 2] = mx_tiles([P, GROUPS, WIDE], "h", 2)
            codes, scales = h_mx[c // 2]
            for g in range(GROUPS):
                quantize(codes[:, g, span(c % 2, CHUNK)], scales[:, g, span(c % 2, CHUNK)], h_cols[c][:, span(g, CHUNK), :])

        def third_product(pair, g, t):
            banks["third", pair, g, t] = psum.tile([P, WIDE], F32, name="bank")
            codes, scales = h_mx[pair]
            c_product(banks["third", pair, g, t][:], g, t, [codes[:, kg, :] for kg in range(GROUPS)],
                      [scales[:, kg, :] for kg in range(GROUPS)])

        def finish_y(pair, g, t):
            y = y_f32[pair, g][:, t, :]
            nc.vector.scalar_tensor_tensor(
                out=y, in0=banks["third", pair, g, t][:], scalar=minus_gain[:, span(g * SLOTS + t, 1)], in1=y,
                op0=ALU.mult, op1=ALU.add,
            )
            dst = out_0[span(g, GROUP), span(pair, WIDE)].rearrange("(p t) m -> p t m", t=SLOTS)
            nc.sync.dma_start(out=dst[:, t, :], in_=y)

        def round_y(c, g, on_vector=False):
            y_cols[c, g] = narrow_stage()
            copy(on_vector, walk_cols(y_cols[c, g][:]), walk_slots(y_f32[c // 2, g][:, :, span(c % 2, CHUNK)]))

        def quantize_y(c, g):
            codes = work.tile([P, CHUNK], U32, name="y_codes", bufs=TEST // CHUNK * GROUPS, align_bytes=64)
            quantize(codes[:], y_scales[SCALE_ROWS * g :, span(c, CHUNK)], y_cols[c, g][:])
            dst = out_1[g, :, span(c, CHUNK), :].rearrange("p m t -> p (m t)")
            nc.sync.dma_start(out=dst.bitcast(I32), in_=codes[:].bitcast(I32))

        def each_bank(step, *key):
            for b in range(BANKS):
                step(*key, b)

        def weave(step, key, between):
            for b in range(BANKS):
                step(*key, b)
                for call in between[b]:
                    call[0](*call[1:])

        nc.vector.memset(c_scales_raw[:].rearrange("p g n -> p (g n)").bitcast(I32), 0)
        for kp in range(PASSES):
            load_rows(f_rows, F, kp, 0)
            if kp == 0:
                load_c_scales()
            load_rows(z_rows, Z, kp, 0)
        last = PASSES - 1
        for kp in range(last):
            load_rows(z_rows, Z, kp, 1)
        load_rows(b_old, B_old, 0, 0)
        load_rows(z_rows, Z, last, 1)
        load_rows(f_rows, F, 0, 1)
        load_rows(b_old, B_old, 1, 0)
        nc.sync.dma_start(out=c_words_raw[:].bitcast(I32), in_=C_words.rearrange("g p b -> p g b").bitcast(I32))
        nc.sync.dma_start(out=gain_raw[:], in_=inv_sd.rearrange("(g p t) -> p g t", g=GROUPS, t=SLOTS))
        late_loads = [(f_rows, F, kp, 1) for kp in range(1, PASSES)] + [(b_old, B_old, g, 1) for g in range(GROUPS)]

        def late_load(index):
            if index < len(late_loads):
                load_rows(*late_loads[index])

        for kp in range(PASSES):
            lay_out_f_wide(kp)
            late_load(2 * kp)
            if kp:
                quantize_z_and_multiply(kp - 1, 0)
            else:
                deal(c_scales[:], c_scales_raw[:])
            lay_out_z(kp, 0)
            late_load(2 * kp + 1)
            quantize_f_wide(kp)
        for kp in range(last):
            lay_out_z(kp, 1)
            quantize_z_and_multiply(*((kp - 1, 1) if kp else (last, 0)))
        weave(add_old_wide, (0, span(0, WIDE)), [
            [(quantize_z_and_multiply, last - 1, 1), (lay_out_z, last, 1)],
            [(quantize_z_and_multiply, last, 1)],
            [],
            [],
        ])

        lay_out_f(2, 0)
        round_b(0, 0)
        each_bank(add_old_wide, 1, span(0, CHUNK))
        round_b(0, 1)
        round_b(1, 0)
        deal(c_words[:].bitcast(U16), c_words_raw[:].bitcast(U16))
        weave(add_old_wide, (1, span(1, CHUNK)), [[], [(quantize_b, 0), (each_bank, second_product, 0)], [], []])
        for kp in range(1, PASSES):
            lay_out_f(2, kp)
        lay_out_f(3, 0)
        lay_out_f(3, 1)
        quantize_f(2, 0)
        round_b(1, 1, on_vector=True)
        gain_flat = gain_raw[:].rearrange("p g t -> p (g t)")
        nc.vector.tensor_copy(out=gain[:], in_=gain_flat)
        nc.vector.tensor_scalar(out=minus_gain[:], in0=gain_flat, scalar1=-1.0, scalar2=None, op0=ALU.mult)
        quantize_b(1)
        each_bank(second_product, 1)
        lay_out_f(3, 2)

        weave(subtract_h, (0,), [[(quantize_f, 2, 1), (lay_out_f, 3, 3)], [(quantize_f, 2, 2)], [], [(quantize_f, 2, 3), (each_bank, first_product, 2)]])
        weave(subtract_h, (1,), [[(quantize_h, 0)], [(quantize_f, 3, 0)], [(quantize_f, 3, 1)], [(quantize_f, 3, 2)]])
        weave(add_old, (2,), [
            [(quantize_f, 3, 3), (first_product, 3, 0), (quantize_h, 1)],
            [(first_product, 3, 1), (scale_b, 0, 0), (round_b, 2, 0)],
            [(first_product, 3, 2)],
            [(first_product, 3, 3), (round_b, 2, 1)],
        ])
        weave(add_old, (3,), [
            [],
            [(quantize_b, 2), (round_b, 3, 0)],
            [],
            [(each_bank, third_product, 0, 0), (round_b, 3, 1), (scale_b, 0, 1), (each_bank, second_product, 2)],
        ])
        each_bank(finish_y, 0, 0)
        round_y(0, 0)
        round_y(1, 0)
        quantize_b(3)
        each_bank(second_product, 3)
        scale_b(1, 0)
        scale_b(1, 1)
        each_bank(subtract_h, 2)
        quantize_y(0, 0)
        each_bank(third_product, 0, 1)
        weave(subtract_h, (3,), [[(quantize_h, 2)], [(quantize_y, 1, 0)], [], []])
        weave(finish_y, (0, 1), [[(quantize_h, 3), (each_bank, third_product, 1, 0)], [], [], []])
        each_bank(third_product, 1, 1)
        round_y(0, 1)
        round_y(1, 1)
        each_bank(finish_y, 1, 0)
        round_y(2, 0)
        round_y(3, 0)
        quantize_y(0, 1)
        weave(finish_y, (1, 1), [[], [(quantize_y, 1, 1)], [], [(quantize_y, 2, 0)]])

        round_y(2, 1)
        round_y(3, 1, on_vector=True)
        quantize_y(3, 0)
        quantize_y(3, 1)
        quantize_y(2, 1)
        for q in range(QUADRANTS):
            nc.scalar.dma_start(
                out=out_2[:, span(q, SCALE_ROWS), :].bitcast(I32),
                in_=y_scales[32 * q : 32 * q + SCALE_ROWS * GROUPS].bitcast(I32),
            )
